import numpy as np, ml_dtypes
CORES = [22,46,70,150,174,198,278,302,326,406,430,454]
N = 12
KB, QP = 2, 64
MEM = [3,9]
def setup_inputs(rng):
    q = rng.standard_normal((N, 128, QP), dtype=np.float32) / 4; k = rng.standard_normal((N, 128, KB * 128), dtype=np.float32)
    a = 2 * np.pi * rng.random((N, QP)); s = 400 * rng.random((N, QP)) ** 1.5; q[:, 0, :] = s * np.cos(a); q[:, 1, :] = s * np.sin(a); q[:, 2, :] = 150 * rng.standard_normal((N, QP)); k[:, 2, :] = 1 + k[:, 2, :] / 50
    c = np.zeros(N); c[MEM] = rng.permutation(len(MEM))
    a = (2 * np.pi * rng.random() + np.pi / 2 * (c.reshape(N, 1, 1) + 0.5) / len(MEM) - 0.5 + (np.arange(KB).reshape(1, KB, 1) + rng.random((N, KB, 128))) / KB).reshape(N, KB * 128); k[:, 0, :] = np.cos(a); k[:, 1, :] = np.sin(a)
    return {"q": q.astype(ml_dtypes.bfloat16), "k": k.astype(ml_dtypes.bfloat16), "v": rng.standard_normal((N, 128, KB * 128), dtype=np.float32).astype(ml_dtypes.bfloat16)}
def setup_inputs_big(rng):
    d = setup_inputs(rng)
    for k in ("v",): d[k] = (d[k].astype(np.float32) * 1048576.0).astype(d[k].dtype)
    return d
def setup_inputs_small(rng):
    d = setup_inputs(rng)
    for k in ("v",): d[k] = (d[k].astype(np.float32) * (1 / 1048576.0)).astype(d[k].dtype)
    return d
def reference(q, k, v):
    Q, K, V = q.astype(np.float64), k.astype(np.float64), v.astype(np.float64)
    y = np.zeros((N, QP, 128))
    for r in range(N):
        js = list(MEM)
        S = np.concatenate([K[j].T @ Q[r] for j in js], axis=0)
        P = np.exp(S - S.max(axis=0)); P = P / P.sum(axis=0)
        y[r] = P.T @ np.concatenate([V[j][:, 128 * b:128 * b + 128] for j in js for b in range(KB)], axis=0)
    return {"y": y.astype(ml_dtypes.bfloat16)}

@@ -1,0 +1,248 @@
+import math
+from concourse.bass import DstId, RemoteDMATransfer
+from concourse.mybir import AluOpType, AxisListType, ActivationFunctionType
+
+QP = 64
+NT = 3
+KEYS = 256
+SLOT = 136
+USED = 130
+STEP = 32.0
+MAGIC = 12582912.0
+EPS = math.exp(-STEP)
+
+SCRATCH = {
+    "qall": ("sbuf", [128, 2 * NT * QP], "bfloat16"),
+    "kbuf": ("sbuf", [128, KEYS], "bfloat16"),
+    "vbuf": ("sbuf", [128, 2 * SLOT], "bfloat16"),
+    "ones": ("sbuf", [128, 128], "bfloat16"),
+    "ident": ("sbuf", [128, 128], "bfloat16"),
+    "land": ("sbuf", [128, 2 * SLOT], "bfloat16"),
+    "mx": ("sbuf", [128, 4], "float32"),
+    "rk": ("sbuf", [128, 4], "float32"),
+    "nb": ("sbuf", [128, 4], "float32"),
+    "km1": ("sbuf", [128, 4], "float32"),
+    "xx": ("sbuf", [128, 4], "float32"),
+    "ww": ("sbuf", [128, 4], "float32"),
+    "ab": ("sbuf", [128, 4], "float32"),
+    "ta": ("sbuf", [128, 132], "float32"),
+    "tt": ("sbuf", [128, 132], "float32"),
+    "rr": ("sbuf", [128, 4], "float32"),
+    "ybuf": ("sbuf", [128, 128], "bfloat16"),
+    "psm": ("psum", [128, 512], "float32"),
+}
+for _t in range(NT):
+    SCRATCH["p%d" % _t] = ("sbuf", [128, KEYS], "bfloat16")
+    SCRATCH["pt%d" % _t] = ("sbuf", [128, KEYS], "bfloat16")
+    SCRATCH["ob%d" % _t] = ("sbuf", [128, SLOT], "bfloat16")
+    SCRATCH["ps%d" % _t] = ("psum", [128, 512], "float32")
+    SCRATCH["pst%d" % _t] = ("psum", [128, 1024], "bfloat16")
+
+SEMAPHORES = ["qld", "ks", "vs", "vone", "idn", "idd", "pa0", "pa1", "loc", "st",
+              "m1", "m2", "m3", "m4", "m5", "m6", "m7", "m8", "m9"]
+for _t in range(NT):
+    SEMAPHORES += ["%s%d" % (_n, _t) for _n in ("qa", "sS", "sM", "sA", "sC", "sB", "sE", "sT", "sP", "sO", "sR")]
+
+
+def _plan(T, topo):
+    cores = list(T.cores)
+    mem = [cores[j] for j in T.tables["MEM"]]
+
+    def rack_of(c):
+        return topo.rack(topo.host(c))
+
+    members = {}
+    for c in cores:
+        members.setdefault(rack_of(c), []).append(c)
+    server = {}
+    for R in members:
+        for s, cj in enumerate(mem):
+            if rack_of(cj) == R:
+                server[(R, s)] = cj
+    for R in members:
+        for s, cj in enumerate(mem):
+            if (R, s) not in server:
+                taken = [server[key] for key in server if key[0] == R]
+                server[(R, s)] = [c for c in members[R] if c not in taken and topo.may_write(cj, c)
+                                  and topo.chip(c) == topo.chip(cj)][0]
+    return mem, members, server, rack_of
+
+
+def rank_program(g, core, T, topo):
+    if T.rank_of(core) is None:
+        return
+    A, AF = AluOpType, ActivationFunctionType
+    mem, members, server, rack_of = _plan(T, topo)
+    R = rack_of(core)
+    mine = members[R]
+    idx = mine.index(core)
+    tile, half = idx // 2, idx % 2
+    srv = [server[(R, s)] for s in range(len(mem))]
+    slot = srv.index(core) if core in srv else None
+    is_mem = core in mem
+    sem = T.sem
+    sent = [0]
+
+    def engines(m):
+        return bin(m).count("1")
+
+    def send(out_ap, in_ap, dsts, remote_sem):
+        m = topo.mask(core, dsts[0])
+        for d in dsts:
+            m &= topo.mask(core, d)
+        if len(dsts) == 1:
+            rid, pid = topo.addr(dsts[0], core)
+            g.remote_dma(out_ap, in_ap, remote_sem, sem.loc, pid, rid, m)
+        else:
+            ids = []
+            for d in dsts:
+                rid, pid = topo.addr(d, core)
+                ids.append(DstId(rid=rid, pnc=pid))
+            g.remote_dma_fused([RemoteDMATransfer(dst_ids=ids, dma_engine_mask=m, remote_sem=remote_sem,
+                                                  srcs=[in_ap], dsts=[out_ap for d in dsts], alu_op=0)],
+                               local_sem=sem.loc)
+        sent[0] += engines(m)
+
+    def arrives(src):
+        return engines(topo.mask(src, core))
+
+    myq = T.qall[:, QP * idx:QP * idx + QP]
+
+    if is_mem:
+        g.sync.dma_start(T.kbuf[:], T.k[:]).then_inc(sem.ks, 16)
+        for b in range(2):
+            g.scalar.dma_start(T.vbuf[:, SLOT * b:SLOT * b + 128], T.v[:, 128 * b:128 * b + 128]).then_inc(sem.vs, 16)
+            g.vector.memset(T.vbuf[:, SLOT * b + 128:SLOT * b + SLOT], 1.0).then_inc(sem.vone, 1)
+    g.sync.dma_start(myq, T.q[:]).then_inc(sem.qld, 16)
+    if slot is not None:
+        g.vector.memset(T.ones[:], 1.0).then_inc(sem.idn, 1)
+        g.wait_ge(sem.idn, 1)
+        g.affine_select(T.ident[:], T.ones[:], [[-1, 128]], A.is_equal, 0.0, 0, 1).then_inc(sem.idd, 1)
+
+    if is_mem:
+        s_own = mem.index(core)
+        copies = [server[(R2, s_own)] for R2 in members if R2 != R]
+        g.wait_ge(sem.ks, 16)
+        for d in copies:
+            send(T.kbuf[:], T.kbuf[:], [d], sem.ks)
+        g.wait_ge(sem.vs, 32)
+        g.wait_ge(sem.vone, 2)
+        for d in copies:
+            send(T.vbuf[:], T.vbuf[:], [d], sem.vs)
+    targets = sorted([d for d in srv if d != core],
+                     key=lambda d: (mine.index(d) // 2 != tile, d not in mem))
+    g.wait_ge(sem.qld, 16)
+    for d in targets:
+        send(myq, myq, [d], sem["qa%d" % tile])
+
+    if slot is not None:
+        other_tiles = [mine.index(d) // 2 for d in srv if d != core]
+        order = sorted(range(NT), key=lambda t: (t != tile, t in other_tiles))
+        holder = mem[slot]
+        k_ready = 16 if is_mem else arrives(holder)
+        v_ready = 32 if is_mem else arrives(holder)
+        pe, dve, act = g.tensor, g.vector, g.scalar
+
+        def res(t):
+            return T.land[:, SLOT * slot:SLOT * slot + SLOT] if t == tile else T["ob%d" % t][:]
+
+        def res_cols(t, a, b):
+            return T.land[:, SLOT * slot + a:SLOT * slot + b] if t == tile else T["ob%d" % t][:, a:b]
+
+        def S(t):
+            for c in mine[2 * t:2 * t + 2]:
+                if c == core:
+                    pe.wait_ge(sem.qld, 16)
+            n = sum(arrives(c) for c in mine[2 * t:2 * t + 2] if c != core)
+            pe.wait_ge(sem["qa%d" % t], n)
+            pe.wait_ge(sem.ks, k_ready)
+            pe.matmul(T["ps%d" % t][:, 0:KEYS], T.qall[:, 128 * t:128 * t + 128], T.kbuf[:], True, True
+                      ).then_inc(sem["sS%d" % t], 1)
+
+        def shift(t):
+            dve.wait_ge(sem["sS%d" % t], 1)
+            dve.tensor_reduce(T.mx[:, t:t + 1], T["ps%d" % t][:, 0:KEYS], AxisListType.X, A.max
+                              ).then_inc(sem["sM%d" % t], 1)
+            dve.wait_ge(sem["sM%d" % t], 1)
+            dve.tensor_scalar(T.rk[:, t:t + 1], T.mx[:, t:t + 1], 1.0 / STEP, MAGIC, A.mult, A.add
+                              ).then_inc(sem["sA%d" % t], 1)
+            dve.wait_ge(sem["sA%d" % t], 1)
+            dve.tensor_scalar(T.nb[:, t:t + 1], T.rk[:, t:t + 1], MAGIC, -STEP, A.subtract, A.mult
+                              ).then_inc(sem["sC%d" % t], 1)
+
+        def step_out(t):
+            dve.tensor_scalar(res_cols(t, 129, 130), T.rk[:, t:t + 1], MAGIC, None, A.subtract
+                              ).then_inc(sem["sB%d" % t], 1)
+
+        def expo(t):
+            act.wait_ge(sem["sC%d" % t], 1)
+            act.activation(T["p%d" % t][:], T["ps%d" % t][:, 0:KEYS], AF.Exp, bias=T.nb[:, t:t + 1], scale=1.0
+                           ).then_inc(sem["sE%d" % t], 1)
+
+        def turn(t):
+            pe.wait_ge(sem.idd, 1)
+            pe.wait_ge(sem["sE%d" % t], 1)
+            for b in range(2):
+                pe.transpose(T["pst%d" % t][:, 128 * b:128 * b + 128], T["p%d" % t][:, 128 * b:128 * b + 128],
+                             T.ident[:]).then_inc(sem["sT%d" % t], 1)
+
+        def turned(t):
+            dve.wait_ge(sem["sT%d" % t], 2)
+            dve.tensor_copy(T["pt%d" % t][:], T["pst%d" % t][:, 0:KEYS]).then_inc(sem["sP%d" % t], 1)
+
+        def PV(t):
+            pe.wait_ge(sem["sP%d" % t], 1)
+            pe.wait_ge(sem.vs, v_ready)
+            if is_mem:
+                pe.wait_ge(sem.vone, 2)
+            pe.matmul(T["ps%d" % t][:, 256:385], T["pt%d" % t][:, 0:128], T.vbuf[:, 0:129], True, False)
+            pe.matmul(T["ps%d" % t][:, 256:385], T["pt%d" % t][:, 128:256], T.vbuf[:, SLOT:SLOT + 129], False, True
+                      ).then_inc(sem["sO%d" % t], 1)
+
+        def out(t):
+            act.wait_ge(sem["sO%d" % t], 1)
+            act.activation(res_cols(t, 0, 129), T["ps%d" % t][:, 256:385], AF.Copy).then_inc(sem["sR%d" % t], 1)
+
+        o0, o1, o2 = order
+        S(o0); S(o1); turn(o0); PV(o0); S(o2); turn(o1); PV(o1); turn(o2); PV(o2)
+        shift(o0); step_out(o0); shift(o1); step_out(o1); turned(o0); shift(o2); turned(o1); step_out(o2); turned(o2)
+        expo(o0); expo(o1); out(o0); expo(o2); out(o1); out(o2)
+
+        for t in order:
+            g.wait_ge(sem["sR%d" % t], 1)
+            g.wait_ge(sem["sB%d" % t], 1)
+            dsts = [c for c in mine[2 * t:2 * t + 2] if c != core]
+            send(T.land[:, SLOT * slot:SLOT * slot + USED], res_cols(t, 0, USED), dsts, sem["pa%d" % slot])
+
+    dve, act = g.vector, g.scalar
+    for q_ in (dve, act):
+        for s in range(2):
+            if s == slot:
+                q_.wait_ge(sem["sR%d" % tile], 1)
+                q_.wait_ge(sem["sB%d" % tile], 1)
+            else:
+                q_.wait_ge(sem["pa%d" % s], arrives(srv[s]))
+    steps = T.land[:, 129:SLOT + 130:SLOT]
+    dve.tensor_scalar(T.km1[:, 0:1], T.land[:, 129:130], T.land[:, SLOT + 129:SLOT + 130], 1.0, A.max, A.subtract
+                      ).then_inc(sem.m1, 1)
+    dve.wait_ge(sem.m1, 1)
+    dve.tensor_scalar(T.xx[:, 0:2], steps, T.km1[:, 0:1], -1.0, A.subtract, A.max).then_inc(sem.m2, 1)
+    dve.wait_ge(sem.m2, 1)
+    dve.tensor_scalar(T.ww[:, 0:2], T.xx[:, 0:2], 1.0, EPS, A.add, A.mult).then_inc(sem.m3, 1)
+    dve.wait_ge(sem.m3, 1)
+    dve.tensor_tensor(T.ab[:, 0:2], T.xx[:, 0:2], T.ww[:, 0:2], A.max).then_inc(sem.m4, 1)
+    dve.wait_ge(sem.m4, 1)
+    act.wait_ge(sem.m4, 1)
+    dve.tensor_scalar(T.ta[:, 0:129], T.land[:, 0:129], T.ab[:, 0:1], None, A.mult).then_inc(sem.m5, 1)
+    act.activation(T.psm[:, 0:129], T.land[:, SLOT:SLOT + 129], AF.Copy, scale=T.ab[:, 1:2]).then_inc(sem.m6, 1)
+    dve.wait_ge(sem.m5, 1)
+    dve.wait_ge(sem.m6, 1)
+    dve.tensor_tensor(T.tt[:, 0:129], T.ta[:, 0:129], T.psm[:, 0:129], A.add).then_inc(sem.m7, 1)
+    dve.wait_ge(sem.m7, 1)
+    dve.reciprocal(T.rr[:, 0:1], T.tt[:, 128:129]).then_inc(sem.m8, 1)
+    dve.wait_ge(sem.m8, 1)
+    dve.tensor_scalar(T.ybuf[:], T.tt[:, 0:128], T.rr[:, 0:1], None, A.mult).then_inc(sem.m9, 1)
+    g.sync.wait_ge(sem.m9, 1)
+    g.sync.dma_start(T.y[:], T.ybuf[QP * half:QP * half + QP, :]).then_inc(sem.st, 16)
+    g.sync.wait_ge(sem.st, 16)
+    g.wait_ge(sem.loc, sent[0])

@@ -4,6 +4,7 @@ from concourse.mybir import AluOpType, AxisListType, ActivationFunctionType
 
 QP = 64
 NT = 3
+LAST = NT - 1
 KEYS = 256
 SLOT = 136
 USED = 130
@@ -15,6 +16,7 @@ SCRATCH = {
     "qall": ("sbuf", [128, 2 * NT * QP], "bfloat16"),
     "kbuf": ("sbuf", [128, KEYS], "bfloat16"),
     "vbuf": ("sbuf", [128, 2 * SLOT], "bfloat16"),
+    "zer": ("sbuf", [128, 128], "bfloat16"),
     "ones": ("sbuf", [128, 128], "bfloat16"),
     "ident": ("sbuf", [128, 128], "bfloat16"),
     "land": ("sbuf", [128, 2 * SLOT], "bfloat16"),
@@ -30,6 +32,7 @@ SCRATCH = {
     "rr": ("sbuf", [128, 4], "float32"),
     "ybuf": ("sbuf", [128, 128], "bfloat16"),
     "psm": ("psum", [128, 512], "float32"),
+    "pstx": ("psum", [128, 1024], "bfloat16"),
 }
 for _t in range(NT):
     SCRATCH["p%d" % _t] = ("sbuf", [128, KEYS], "bfloat16")
@@ -38,8 +41,8 @@ for _t in range(NT):
     SCRATCH["ps%d" % _t] = ("psum", [128, 512], "float32")
     SCRATCH["pst%d" % _t] = ("psum", [128, 1024], "bfloat16")
 
-SEMAPHORES = ["qld", "ks", "vs", "vone", "idn", "idd", "pa0", "pa1", "loc", "st",
-              "m1", "m2", "m3", "m4", "m5", "m6", "m7", "m8", "m9"]
+SEMAPHORES = ["zr", "qld", "ks", "vs", "vone", "idn", "idd", "pa0", "pa1", "loc", "st",
+              "m1", "m2", "m3", "m4", "m5", "m6", "m7", "m8", "m9", "xE0", "xE1", "xT0", "xT1", "xP0", "xP1"]
 for _t in range(NT):
     SEMAPHORES += ["%s%d" % (_n, _t) for _n in ("qa", "sS", "sM", "sA", "sC", "sB", "sE", "sT", "sP", "sO", "sR")]
 
@@ -74,10 +77,10 @@ def rank_program(g, core, T, topo):
     A, AF = AluOpType, ActivationFunctionType
     mem, members, server, rack_of = _plan(T, topo)
     R = rack_of(core)
-    mine = members[R]
+    srv = [server[(R, s)] for s in range(len(mem))]
+    mine = [c for c in members[R] if c not in srv] + srv
     idx = mine.index(core)
     tile, half = idx // 2, idx % 2
-    srv = [server[(R, s)] for s in range(len(mem))]
     slot = srv.index(core) if core in srv else None
     is_mem = core in mem
     sem = T.sem
@@ -106,6 +109,10 @@ def rank_program(g, core, T, topo):
     def arrives(src):
         return engines(topo.mask(src, core))
 
+    def tile_order(server_core):
+        first = list(range(LAST))
+        return (first if server_core in mem else first[::-1]) + [LAST]
+
     myq = T.qall[:, QP * idx:QP * idx + QP]
 
     if is_mem:
@@ -115,9 +122,9 @@ def rank_program(g, core, T, topo):
             g.vector.memset(T.vbuf[:, SLOT * b + 128:SLOT * b + SLOT], 1.0).then_inc(sem.vone, 1)
     g.sync.dma_start(myq, T.q[:]).then_inc(sem.qld, 16)
     if slot is not None:
-        g.vector.memset(T.ones[:], 1.0).then_inc(sem.idn, 1)
-        g.wait_ge(sem.idn, 1)
-        g.affine_select(T.ident[:], T.ones[:], [[-1, 128]], A.is_equal, 0.0, 0, 1).then_inc(sem.idd, 1)
+        g.vector.memset(T.zer[:], 0.0).then_inc(sem.zr, 1)
+        g.scalar.wait_ge(sem.zr, 1)
+        g.scalar.activation(T.ones[:], T.zer[:], AF.Exp).then_inc(sem.idn, 1)
 
     if is_mem:
         s_own = mem.index(core)
@@ -129,22 +136,20 @@ def rank_program(g, core, T, topo):
         g.wait_ge(sem.vone, 2)
         for d in copies:
             send(T.vbuf[:], T.vbuf[:], [d], sem.vs)
-    targets = sorted([d for d in srv if d != core],
-                     key=lambda d: (mine.index(d) // 2 != tile, d not in mem))
+    targets = sorted([d for d in srv if d != core], key=lambda d: tile_order(d).index(tile))
     g.wait_ge(sem.qld, 16)
     for d in targets:
         send(myq, myq, [d], sem["qa%d" % tile])
+    if slot is not None:
+        g.wait_ge(sem.idn, 1)
+        g.affine_select(T.ident[:], T.ones[:], [[-1, 128]], A.is_equal, 0.0, 0, 1).then_inc(sem.idd, 1)
 
     if slot is not None:
-        other_tiles = [mine.index(d) // 2 for d in srv if d != core]
-        order = sorted(range(NT), key=lambda t: (t != tile, t in other_tiles))
+        order = tile_order(core)
         holder = mem[slot]
         k_ready = 16 if is_mem else arrives(holder)
         v_ready = 32 if is_mem else arrives(holder)
         pe, dve, act = g.tensor, g.vector, g.scalar
-
-        def res(t):
-            return T.land[:, SLOT * slot:SLOT * slot + SLOT] if t == tile else T["ob%d" % t][:]
 
         def res_cols(t, a, b):
             return T.land[:, SLOT * slot + a:SLOT * slot + b] if t == tile else T["ob%d" % t][:, a:b]
@@ -190,11 +195,14 @@ def rank_program(g, core, T, topo):
             dve.wait_ge(sem["sT%d" % t], 2)
             dve.tensor_copy(T["pt%d" % t][:], T["pst%d" % t][:, 0:KEYS]).then_inc(sem["sP%d" % t], 1)
 
-        def PV(t):
-            pe.wait_ge(sem["sP%d" % t], 1)
+        def v_wait():
             pe.wait_ge(sem.vs, v_ready)
             if is_mem:
                 pe.wait_ge(sem.vone, 2)
+
+        def PV(t):
+            pe.wait_ge(sem["sP%d" % t], 1)
+            v_wait()
             pe.matmul(T["ps%d" % t][:, 256:385], T["pt%d" % t][:, 0:128], T.vbuf[:, 0:129], True, False)
             pe.matmul(T["ps%d" % t][:, 256:385], T["pt%d" % t][:, 128:256], T.vbuf[:, SLOT:SLOT + 129], False, True
                       ).then_inc(sem["sO%d" % t], 1)
@@ -203,10 +211,35 @@ def rank_program(g, core, T, topo):
             act.wait_ge(sem["sO%d" % t], 1)
             act.activation(res_cols(t, 0, 129), T["ps%d" % t][:, 256:385], AF.Copy).then_inc(sem["sR%d" % t], 1)
 
-        o0, o1, o2 = order
-        S(o0); S(o1); turn(o0); PV(o0); S(o2); turn(o1); PV(o1); turn(o2); PV(o2)
-        shift(o0); step_out(o0); shift(o1); step_out(o1); turned(o0); shift(o2); turned(o1); step_out(o2); turned(o2)
-        expo(o0); expo(o1); out(o0); expo(o2); out(o1); out(o2)
+        t2 = LAST
+        bank = [T["pst%d" % t2], T.pstx]
+
+        def expo_b(b):
+            act.wait_ge(sem["sC%d" % t2], 1)
+            act.activation(T["p%d" % t2][:, 128 * b:128 * b + 128], T["ps%d" % t2][:, 128 * b:128 * b + 128], AF.Exp,
+                           bias=T.nb[:, t2:t2 + 1], scale=1.0).then_inc(sem["xE%d" % b], 1)
+
+        def turn_b(b):
+            pe.wait_ge(sem["xE%d" % b], 1)
+            pe.transpose(bank[b][:, 0:128], T["p%d" % t2][:, 128 * b:128 * b + 128], T.ident[:]
+                         ).then_inc(sem["xT%d" % b], 1)
+
+        def turned_b(b):
+            dve.wait_ge(sem["xT%d" % b], 1)
+            dve.tensor_copy(T["pt%d" % t2][:, 128 * b:128 * b + 128], bank[b][:, 0:128]).then_inc(sem["xP%d" % b], 1)
+
+        def PV_b(b):
+            pe.wait_ge(sem["xP%d" % b], 1)
+            i = pe.matmul(T["ps%d" % t2][:, 256:385], T["pt%d" % t2][:, 128 * b:128 * b + 128],
+                          T.vbuf[:, SLOT * b:SLOT * b + 129], b == 0, b == 1)
+            if b == 1:
+                i.then_inc(sem["sO%d" % t2], 1)
+
+        o0, o1 = order[0], order[1]
+        S(o0); S(o1); turn(o0); PV(o0); S(t2); turn(o1); PV(o1); turn_b(0); turn_b(1); PV_b(0); PV_b(1)
+        shift(o0); step_out(o0); shift(o1); step_out(o1); turned(o0); shift(t2); turned(o1); step_out(t2)
+        turned_b(0); turned_b(1)
+        expo(o0); expo(o1); out(o0); expo_b(0); expo_b(1); out(o1); out(t2)
 
         for t in order:
             g.wait_ge(sem["sR%d" % t], 1)

@@ -11,6 +11,7 @@ USED = 130
 STEP = 32.0
 MAGIC = 12582912.0
 EPS = math.exp(-STEP)
+NQ, NK, NR = 8, 8, 8
 
 SCRATCH = {
     "qall": ("sbuf", [128, 2 * NT * QP], "bfloat16"),
@@ -32,19 +33,20 @@ SCRATCH = {
     "rr": ("sbuf", [128, 4], "float32"),
     "ybuf": ("sbuf", [128, 128], "bfloat16"),
     "psm": ("psum", [128, 512], "float32"),
-    "pstx": ("psum", [128, 1024], "bfloat16"),
 }
 for _t in range(NT):
     SCRATCH["p%d" % _t] = ("sbuf", [128, KEYS], "bfloat16")
     SCRATCH["pt%d" % _t] = ("sbuf", [128, KEYS], "bfloat16")
     SCRATCH["ob%d" % _t] = ("sbuf", [128, SLOT], "bfloat16")
     SCRATCH["ps%d" % _t] = ("psum", [128, 512], "float32")
+for _t in range(4):
     SCRATCH["pst%d" % _t] = ("psum", [128, 1024], "bfloat16")
 
 SEMAPHORES = ["zr", "qld", "ks", "vs", "vone", "idn", "idd", "pa0", "pa1", "loc", "st",
-              "m1", "m2", "m3", "m4", "m5", "m6", "m7", "m8", "m9", "xE0", "xE1", "xT0", "xT1", "xP0", "xP1"]
+              "m1", "m2", "m3", "m4", "m5", "m6", "m7", "m8", "m9"]
 for _t in range(NT):
-    SEMAPHORES += ["%s%d" % (_n, _t) for _n in ("qa", "sS", "sM", "sA", "sC", "sB", "sE", "sT", "sP", "sO", "sR")]
+    SEMAPHORES += ["%s%d" % (_n, _t) for _n in ("qa", "sS", "sM", "sA", "sC", "sB", "sO", "sR")]
+    SEMAPHORES += ["%s%d%d" % (_n, _t, _b) for _n in ("xE", "xT", "xP") for _b in range(2)]
 
 
 def _plan(T, topo):
@@ -86,13 +88,15 @@ def rank_program(g, core, T, topo):
     sem = T.sem
     sent = [0]
 
-    def engines(m):
-        return bin(m).count("1")
+    def pick(m, n):
+        bits = [e for e in range(16) if (m >> e) & 1][:n]
+        return sum(1 << e for e in bits)
 
-    def send(out_ap, in_ap, dsts, remote_sem):
+    def send(out_ap, in_ap, dsts, remote_sem, n):
         m = topo.mask(core, dsts[0])
         for d in dsts:
             m &= topo.mask(core, d)
+        m = pick(m, n)
         if len(dsts) == 1:
             rid, pid = topo.addr(dsts[0], core)
             g.remote_dma(out_ap, in_ap, remote_sem, sem.loc, pid, rid, m)
@@ -104,10 +108,7 @@ def rank_program(g, core, T, topo):
             g.remote_dma_fused([RemoteDMATransfer(dst_ids=ids, dma_engine_mask=m, remote_sem=remote_sem,
                                                   srcs=[in_ap], dsts=[out_ap for d in dsts], alu_op=0)],
                                local_sem=sem.loc)
-        sent[0] += engines(m)
-
-    def arrives(src):
-        return engines(topo.mask(src, core))
+        sent[0] += n
 
     def tile_order(server_core):
         first = list(range(LAST))
@@ -117,39 +118,43 @@ def rank_program(g, core, T, topo):
 
     if is_mem:
         g.sync.dma_start(T.kbuf[:], T.k[:]).then_inc(sem.ks, 16)
+        g.scalar.dma_start(myq, T.q[:]).then_inc(sem.qld, 16)
         for b in range(2):
-            g.scalar.dma_start(T.vbuf[:, SLOT * b:SLOT * b + 128], T.v[:, 128 * b:128 * b + 128]).then_inc(sem.vs, 16)
+            g.sync.dma_start(T.vbuf[:, SLOT * b:SLOT * b + 128], T.v[:, 128 * b:128 * b + 128]).then_inc(sem.vs, 16)
             g.vector.memset(T.vbuf[:, SLOT * b + 128:SLOT * b + SLOT], 1.0).then_inc(sem.vone, 1)
-    g.sync.dma_start(myq, T.q[:]).then_inc(sem.qld, 16)
+    else:
+        g.sync.dma_start(myq, T.q[:]).then_inc(sem.qld, 16)
     if slot is not None:
         g.vector.memset(T.zer[:], 0.0).then_inc(sem.zr, 1)
         g.scalar.wait_ge(sem.zr, 1)
         g.scalar.activation(T.ones[:], T.zer[:], AF.Exp).then_inc(sem.idn, 1)
 
+    copies = []
     if is_mem:
-        s_own = mem.index(core)
-        copies = [server[(R2, s_own)] for R2 in members if R2 != R]
+        copies = [server[(R2, mem.index(core))] for R2 in members if R2 != R]
         g.wait_ge(sem.ks, 16)
         for d in copies:
-            send(T.kbuf[:], T.kbuf[:], [d], sem.ks)
-        g.wait_ge(sem.vs, 32)
-        g.wait_ge(sem.vone, 2)
-        for d in copies:
-            send(T.vbuf[:], T.vbuf[:], [d], sem.vs)
+            send(T.kbuf[:], T.kbuf[:], [d], sem.ks, NK)
     targets = sorted([d for d in srv if d != core], key=lambda d: tile_order(d).index(tile))
     g.wait_ge(sem.qld, 16)
     for d in targets:
-        send(myq, myq, [d], sem["qa%d" % tile])
+        send(myq, myq, [d], sem["qa%d" % tile], NQ)
+    if is_mem:
+        g.wait_ge(sem.vs, 32)
+        g.wait_ge(sem.vone, 2)
+        for d in copies:
+            send(T.vbuf[:], T.vbuf[:], [d], sem.vs, NK)
     if slot is not None:
         g.wait_ge(sem.idn, 1)
         g.affine_select(T.ident[:], T.ones[:], [[-1, 128]], A.is_equal, 0.0, 0, 1).then_inc(sem.idd, 1)
 
     if slot is not None:
         order = tile_order(core)
-        holder = mem[slot]
-        k_ready = 16 if is_mem else arrives(holder)
-        v_ready = 32 if is_mem else arrives(holder)
+        o0, o1, o2 = order
+        k_ready = 16 if is_mem else NK
+        v_ready = 32 if is_mem else NK
         pe, dve, act = g.tensor, g.vector, g.scalar
+        bank = {(o0, 0): T.pst0, (o0, 1): T.pst1, (o1, 0): T.pst2, (o1, 1): T.pst3, (o2, 0): T.pst0, (o2, 1): T.pst1}
 
         def res_cols(t, a, b):
             return T.land[:, SLOT * slot + a:SLOT * slot + b] if t == tile else T["ob%d" % t][:, a:b]
@@ -158,94 +163,73 @@ def rank_program(g, core, T, topo):
             for c in mine[2 * t:2 * t + 2]:
                 if c == core:
                     pe.wait_ge(sem.qld, 16)
-            n = sum(arrives(c) for c in mine[2 * t:2 * t + 2] if c != core)
-            pe.wait_ge(sem["qa%d" % t], n)
+            pe.wait_ge(sem["qa%d" % t], NQ * len([c for c in mine[2 * t:2 * t + 2] if c != core]))
             pe.wait_ge(sem.ks, k_ready)
             pe.matmul(T["ps%d" % t][:, 0:KEYS], T.qall[:, 128 * t:128 * t + 128], T.kbuf[:], True, True
                       ).then_inc(sem["sS%d" % t], 1)
 
-        def shift(t):
+        def top(t):
             dve.wait_ge(sem["sS%d" % t], 1)
             dve.tensor_reduce(T.mx[:, t:t + 1], T["ps%d" % t][:, 0:KEYS], AxisListType.X, A.max
                               ).then_inc(sem["sM%d" % t], 1)
+
+        def whole(t):
             dve.wait_ge(sem["sM%d" % t], 1)
             dve.tensor_scalar(T.rk[:, t:t + 1], T.mx[:, t:t + 1], 1.0 / STEP, MAGIC, A.mult, A.add
                               ).then_inc(sem["sA%d" % t], 1)
+
+        def bias(t):
             dve.wait_ge(sem["sA%d" % t], 1)
             dve.tensor_scalar(T.nb[:, t:t + 1], T.rk[:, t:t + 1], MAGIC, -STEP, A.subtract, A.mult
                               ).then_inc(sem["sC%d" % t], 1)
 
         def step_out(t):
+            dve.wait_ge(sem["sA%d" % t], 1)
             dve.tensor_scalar(res_cols(t, 129, 130), T.rk[:, t:t + 1], MAGIC, None, A.subtract
                               ).then_inc(sem["sB%d" % t], 1)
 
-        def expo(t):
+        def expo(t, b):
             act.wait_ge(sem["sC%d" % t], 1)
-            act.activation(T["p%d" % t][:], T["ps%d" % t][:, 0:KEYS], AF.Exp, bias=T.nb[:, t:t + 1], scale=1.0
-                           ).then_inc(sem["sE%d" % t], 1)
+            act.activation(T["p%d" % t][:, 128 * b:128 * b + 128], T["ps%d" % t][:, 128 * b:128 * b + 128], AF.Exp,
+                           bias=T.nb[:, t:t + 1], scale=1.0).then_inc(sem["xE%d%d" % (t, b)], 1)
 
-        def turn(t):
+        def turn(t, b):
             pe.wait_ge(sem.idd, 1)
-            pe.wait_ge(sem["sE%d" % t], 1)
-            for b in range(2):
-                pe.transpose(T["pst%d" % t][:, 128 * b:128 * b + 128], T["p%d" % t][:, 128 * b:128 * b + 128],
-                             T.ident[:]).then_inc(sem["sT%d" % t], 1)
+            pe.wait_ge(sem["xE%d%d" % (t, b)], 1)
+            pe.transpose(bank[(t, b)][:, 0:128], T["p%d" % t][:, 128 * b:128 * b + 128], T.ident[:]
+                         ).then_inc(sem["xT%d%d" % (t, b)], 1)
 
-        def turned(t):
-            dve.wait_ge(sem["sT%d" % t], 2)
-            dve.tensor_copy(T["pt%d" % t][:], T["pst%d" % t][:, 0:KEYS]).then_inc(sem["sP%d" % t], 1)
+        def turned(t, b):
+            dve.wait_ge(sem["xT%d%d" % (t, b)], 1)
+            dve.tensor_copy(T["pt%d" % t][:, 128 * b:128 * b + 128], bank[(t, b)][:, 0:128]
+                            ).then_inc(sem["xP%d%d" % (t, b)], 1)
 
-        def v_wait():
+        def PV(t, b):
+            pe.wait_ge(sem["xP%d%d" % (t, b)], 1)
             pe.wait_ge(sem.vs, v_ready)
             if is_mem:
                 pe.wait_ge(sem.vone, 2)
-
-        def PV(t):
-            pe.wait_ge(sem["sP%d" % t], 1)
-            v_wait()
-            pe.matmul(T["ps%d" % t][:, 256:385], T["pt%d" % t][:, 0:128], T.vbuf[:, 0:129], True, False)
-            pe.matmul(T["ps%d" % t][:, 256:385], T["pt%d" % t][:, 128:256], T.vbuf[:, SLOT:SLOT + 129], False, True
-                      ).then_inc(sem["sO%d" % t], 1)
+            i = pe.matmul(T["ps%d" % t][:, 256:385], T["pt%d" % t][:, 128 * b:128 * b + 128],
+                          T.vbuf[:, SLOT * b:SLOT * b + 129], b == 0, b == 1)
+            if b == 1:
+                i.then_inc(sem["sO%d" % t], 1)
 
         def out(t):
             act.wait_ge(sem["sO%d" % t], 1)
             act.activation(res_cols(t, 0, 129), T["ps%d" % t][:, 256:385], AF.Copy).then_inc(sem["sR%d" % t], 1)
 
-        t2 = LAST
-        bank = [T["pst%d" % t2], T.pstx]
-
-        def expo_b(b):
-            act.wait_ge(sem["sC%d" % t2], 1)
-            act.activation(T["p%d" % t2][:, 128 * b:128 * b + 128], T["ps%d" % t2][:, 128 * b:128 * b + 128], AF.Exp,
-                           bias=T.nb[:, t2:t2 + 1], scale=1.0).then_inc(sem["xE%d" % b], 1)
-
-        def turn_b(b):
-            pe.wait_ge(sem["xE%d" % b], 1)
-            pe.transpose(bank[b][:, 0:128], T["p%d" % t2][:, 128 * b:128 * b + 128], T.ident[:]
-                         ).then_inc(sem["xT%d" % b], 1)
-
-        def turned_b(b):
-            dve.wait_ge(sem["xT%d" % b], 1)
-            dve.tensor_copy(T["pt%d" % t2][:, 128 * b:128 * b + 128], bank[b][:, 0:128]).then_inc(sem["xP%d" % b], 1)
-
-        def PV_b(b):
-            pe.wait_ge(sem["xP%d" % b], 1)
-            i = pe.matmul(T["ps%d" % t2][:, 256:385], T["pt%d" % t2][:, 128 * b:128 * b + 128],
-                          T.vbuf[:, SLOT * b:SLOT * b + 129], b == 0, b == 1)
-            if b == 1:
-                i.then_inc(sem["sO%d" % t2], 1)
-
-        o0, o1 = order[0], order[1]
-        S(o0); S(o1); turn(o0); PV(o0); S(t2); turn(o1); PV(o1); turn_b(0); turn_b(1); PV_b(0); PV_b(1)
-        shift(o0); step_out(o0); shift(o1); step_out(o1); turned(o0); shift(t2); turned(o1); step_out(t2)
-        turned_b(0); turned_b(1)
-        expo(o0); expo(o1); out(o0); expo_b(0); expo_b(1); out(o1); out(t2)
+        S(o0); S(o1); S(o2); turn(o0, 0); turn(o0, 1); turn(o1, 0); turn(o1, 1)
+        PV(o0, 0); PV(o0, 1); PV(o1, 0); PV(o1, 1); turn(o2, 0); turn(o2, 1); PV(o2, 0); PV(o2, 1)
+        top(o0); whole(o0); bias(o0); top(o1); whole(o1); bias(o1); turned(o0, 0); turned(o0, 1); step_out(o0)
+        top(o2); turned(o1, 0); whole(o2); turned(o1, 1); bias(o2); step_out(o1); step_out(o2)
+        turned(o2, 0); turned(o2, 1)
+        expo(o0, 0); expo(o0, 1); expo(o1, 0); expo(o1, 1); out(o0); expo(o2, 0); expo(o2, 1); out(o1); out(o2)
 
         for t in order:
             g.wait_ge(sem["sR%d" % t], 1)
             g.wait_ge(sem["sB%d" % t], 1)
             dsts = [c for c in mine[2 * t:2 * t + 2] if c != core]
-            send(T.land[:, SLOT * slot:SLOT * slot + USED], res_cols(t, 0, USED), dsts, sem["pa%d" % slot])
+            send(T.land[:, SLOT * slot:SLOT * slot + USED], res_cols(t, 0, USED), dsts, sem["pa%d" % slot], NR)
 
     dve, act = g.vector, g.scalar
     for q_ in (dve, act):
@@ -254,7 +238,7 @@ def rank_program(g, core, T, topo):
                 q_.wait_ge(sem["sR%d" % tile], 1)
                 q_.wait_ge(sem["sB%d" % tile], 1)
             else:
-                q_.wait_ge(sem["pa%d" % s], arrives(srv[s]))
+                q_.wait_ge(sem["pa%d" % s], NR)
     steps = T.land[:, 129:SLOT + 130:SLOT]
     dve.tensor_scalar(T.km1[:, 0:1], T.land[:, 129:130], T.land[:, SLOT + 129:SLOT + 130], 1.0, A.max, A.subtract
                       ).then_inc(sem.m1, 1)

@@ -1,4 +1,3 @@
-import math
 from concourse.bass import DstId, RemoteDMATransfer
 from concourse.mybir import AluOpType, AxisListType, ActivationFunctionType
 
@@ -7,29 +6,25 @@ NT = 3
 LAST = NT - 1
 KEYS = 256
 SLOT = 136
-USED = 130
-STEP = 32.0
-MAGIC = 12582912.0
-EPS = math.exp(-STEP)
+WIN = QP + 2
 NQ, NK, NR = 8, 8, 8
 
 SCRATCH = {
     "qall": ("sbuf", [128, 2 * NT * QP], "bfloat16"),
     "kbuf": ("sbuf", [128, KEYS], "bfloat16"),
-    "vbuf": ("sbuf", [128, 2 * SLOT], "bfloat16"),
+    "vbuf": ("sbuf", [128, KEYS], "bfloat16"),
     "zer": ("sbuf", [128, 128], "bfloat16"),
     "ones": ("sbuf", [128, 128], "bfloat16"),
     "ident": ("sbuf", [128, 128], "bfloat16"),
     "land": ("sbuf", [128, 2 * SLOT], "bfloat16"),
-    "mx": ("sbuf", [128, 4], "float32"),
-    "rk": ("sbuf", [128, 4], "float32"),
-    "nb": ("sbuf", [128, 4], "float32"),
-    "km1": ("sbuf", [128, 4], "float32"),
-    "xx": ("sbuf", [128, 4], "float32"),
-    "ww": ("sbuf", [128, 4], "float32"),
+    "nb": ("sbuf", [128, 8], "bfloat16"),
+    "ls": ("sbuf", [128, 8], "float32"),
+    "nm": ("sbuf", [128, 4], "float32"),
     "ab": ("sbuf", [128, 4], "float32"),
-    "ta": ("sbuf", [128, 132], "float32"),
-    "tt": ("sbuf", [128, 132], "float32"),
+    "lw": ("sbuf", [128, 4], "float32"),
+    "lt": ("sbuf", [128, 4], "float32"),
+    "ta": ("sbuf", [128, 128], "float32"),
+    "tt": ("sbuf", [128, 128], "float32"),
     "rr": ("sbuf", [128, 4], "float32"),
     "ybuf": ("sbuf", [128, 128], "bfloat16"),
     "psm": ("psum", [128, 512], "float32"),
@@ -42,10 +37,10 @@ for _t in range(NT):
 for _t in range(4):
     SCRATCH["pst%d" % _t] = ("psum", [128, 1024], "bfloat16")
 
-SEMAPHORES = ["zr", "qld", "ks", "vs", "vone", "idn", "idd", "pa0", "pa1", "loc", "st",
-              "m1", "m2", "m3", "m4", "m5", "m6", "m7", "m8", "m9"]
+SEMAPHORES = ["zr", "qld", "ks", "vs", "idn", "idd", "pa0", "pa1", "loc", "st", "lz", "sLo", "sBo", "tT0", "tT1",
+              "m1", "m4", "m5", "m6", "m7", "m8", "m9", "mA", "mB"]
 for _t in range(NT):
-    SEMAPHORES += ["%s%d" % (_n, _t) for _n in ("qa", "sS", "sM", "sA", "sC", "sB", "sO", "sR")]
+    SEMAPHORES += ["%s%d" % (_n, _t) for _n in ("qa", "sS", "sC", "sB", "sL", "sO", "sR")]
     SEMAPHORES += ["%s%d%d" % (_n, _t, _b) for _n in ("xE", "xT", "xP") for _b in range(2)]
 
 
@@ -87,77 +82,86 @@ def rank_program(g, core, T, topo):
     is_mem = core in mem
     sem = T.sem
     sent = [0]
+    pe, dve, act = g.tensor, g.vector, g.scalar
 
-    def pick(m, n):
-        bits = [e for e in range(16) if (m >> e) & 1][:n]
-        return sum(1 << e for e in bits)
-
-    def send(out_ap, in_ap, dsts, remote_sem, n):
+    def engines(dsts):
         m = topo.mask(core, dsts[0])
         for d in dsts:
             m &= topo.mask(core, d)
-        m = pick(m, n)
-        if len(dsts) == 1:
-            rid, pid = topo.addr(dsts[0], core)
-            g.remote_dma(out_ap, in_ap, remote_sem, sem.loc, pid, rid, m)
-        else:
-            ids = []
-            for d in dsts:
-                rid, pid = topo.addr(d, core)
-                ids.append(DstId(rid=rid, pnc=pid))
-            g.remote_dma_fused([RemoteDMATransfer(dst_ids=ids, dma_engine_mask=m, remote_sem=remote_sem,
-                                                  srcs=[in_ap], dsts=[out_ap for d in dsts], alu_op=0)],
-                               local_sem=sem.loc)
+        return [e for e in range(16) if (m >> e) & 1]
+
+    def bits(es):
+        return sum(1 << e for e in es)
+
+    def send(out_ap, in_ap, d, remote_sem, n):
+        rid, pid = topo.addr(d, core)
+        g.remote_dma(out_ap, in_ap, remote_sem, sem.loc, pid, rid, bits(engines([d])[:n]))
         sent[0] += n
+
+    def send_each(parts, remote_sem, n):
+        es = engines([d for _o, _i, d in parts])[:n]
+        share = n // len(parts)
+        trs = []
+        for j, (o_ap, i_ap, d) in enumerate(parts):
+            rid, pid = topo.addr(d, core)
+            trs.append(RemoteDMATransfer(dst_ids=[DstId(rid=rid, pnc=pid)],
+                                         dma_engine_mask=bits(es[share * j:share * j + share]),
+                                         remote_sem=remote_sem, srcs=[i_ap], dsts=[o_ap], alu_op=0))
+        g.remote_dma_fused(trs, local_sem=sem.loc)
+        sent[0] += share * len(parts)
 
     def tile_order(server_core):
         first = list(range(LAST))
         return (first if server_core in mem else first[::-1]) + [LAST]
 
+    def lands(s, h):
+        return T.land[:, SLOT * s:SLOT * s + WIN] if h == 0 else T.land[:, SLOT * s + QP:SLOT * s + QP + WIN]
+
     myq = T.qall[:, QP * idx:QP * idx + QP]
+    lc = 0 if half == 0 else 2 * QP
+    kc = lc + 1
+    others = [s for s in range(2) if s != slot]
 
     if is_mem:
         g.sync.dma_start(T.kbuf[:], T.k[:]).then_inc(sem.ks, 16)
         g.scalar.dma_start(myq, T.q[:]).then_inc(sem.qld, 16)
-        for b in range(2):
-            g.sync.dma_start(T.vbuf[:, SLOT * b:SLOT * b + 128], T.v[:, 128 * b:128 * b + 128]).then_inc(sem.vs, 16)
-            g.vector.memset(T.vbuf[:, SLOT * b + 128:SLOT * b + SLOT], 1.0).then_inc(sem.vone, 1)
+        g.sync.dma_start(T.vbuf[:], T.v[:]).then_inc(sem.vs, 16)
     else:
         g.sync.dma_start(myq, T.q[:]).then_inc(sem.qld, 16)
-    if slot is not None:
-        g.vector.memset(T.zer[:], 0.0).then_inc(sem.zr, 1)
-        g.scalar.wait_ge(sem.zr, 1)
-        g.scalar.activation(T.ones[:], T.zer[:], AF.Exp).then_inc(sem.idn, 1)
+    dve.memset(T.zer[:], 0.0).then_inc(sem.zr, 1)
+    act.wait_ge(sem.zr, 1)
+    act.activation(T.ones[:], T.zer[:], AF.Exp).then_inc(sem.idn, 1)
+    if half == 1:
+        for s in others:
+            dve.memset(T.land[:, SLOT * s:SLOT * s + QP], 0.0).then_inc(sem.lz, 1)
 
     copies = []
     if is_mem:
         copies = [server[(R2, mem.index(core))] for R2 in members if R2 != R]
         g.wait_ge(sem.ks, 16)
         for d in copies:
-            send(T.kbuf[:], T.kbuf[:], [d], sem.ks, NK)
+            send(T.kbuf[:], T.kbuf[:], d, sem.ks, NK)
     targets = sorted([d for d in srv if d != core], key=lambda d: tile_order(d).index(tile))
     g.wait_ge(sem.qld, 16)
     for d in targets:
-        send(myq, myq, [d], sem["qa%d" % tile], NQ)
+        send(myq, myq, d, sem["qa%d" % tile], NQ)
     if is_mem:
-        g.wait_ge(sem.vs, 32)
-        g.wait_ge(sem.vone, 2)
+        g.wait_ge(sem.vs, 16)
         for d in copies:
-            send(T.vbuf[:], T.vbuf[:], [d], sem.vs, NK)
-    if slot is not None:
-        g.wait_ge(sem.idn, 1)
-        g.affine_select(T.ident[:], T.ones[:], [[-1, 128]], A.is_equal, 0.0, 0, 1).then_inc(sem.idd, 1)
+            send(T.vbuf[:], T.vbuf[:], d, sem.vs, NK)
+    g.wait_ge(sem.idn, 1)
+    g.affine_select(T.ident[:], T.ones[:], [[-1, 128]], A.is_equal, 0.0, 0, 1).then_inc(sem.idd, 1)
+
+    turned_bank = {0: T.ps0, 1: T.ps1}
 
     if slot is not None:
         order = tile_order(core)
         o0, o1, o2 = order
         k_ready = 16 if is_mem else NK
-        v_ready = 32 if is_mem else NK
-        pe, dve, act = g.tensor, g.vector, g.scalar
+        v_ready = 16 if is_mem else NK
+        hp = 1 - half
         bank = {(o0, 0): T.pst0, (o0, 1): T.pst1, (o1, 0): T.pst2, (o1, 1): T.pst3, (o2, 0): T.pst0, (o2, 1): T.pst1}
-
-        def res_cols(t, a, b):
-            return T.land[:, SLOT * slot + a:SLOT * slot + b] if t == tile else T["ob%d" % t][:, a:b]
+        turned_bank = {slot: T["ps%d" % o0], 1 - slot: T["ps%d" % o1]}
 
         def S(t):
             for c in mine[2 * t:2 * t + 2]:
@@ -170,28 +174,35 @@ def rank_program(g, core, T, topo):
 
         def top(t):
             dve.wait_ge(sem["sS%d" % t], 1)
-            dve.tensor_reduce(T.mx[:, t:t + 1], T["ps%d" % t][:, 0:KEYS], AxisListType.X, A.max
-                              ).then_inc(sem["sM%d" % t], 1)
-
-        def whole(t):
-            dve.wait_ge(sem["sM%d" % t], 1)
-            dve.tensor_scalar(T.rk[:, t:t + 1], T.mx[:, t:t + 1], 1.0 / STEP, MAGIC, A.mult, A.add
-                              ).then_inc(sem["sA%d" % t], 1)
-
-        def bias(t):
-            dve.wait_ge(sem["sA%d" % t], 1)
-            dve.tensor_scalar(T.nb[:, t:t + 1], T.rk[:, t:t + 1], MAGIC, -STEP, A.subtract, A.mult
+            dve.tensor_reduce(T.nb[:, t:t + 1], T["ps%d" % t][:, 0:KEYS], AxisListType.X, A.max, negate=True
                               ).then_inc(sem["sC%d" % t], 1)
 
         def step_out(t):
-            dve.wait_ge(sem["sA%d" % t], 1)
-            dve.tensor_scalar(res_cols(t, 129, 130), T.rk[:, t:t + 1], MAGIC, None, A.subtract
+            dve.wait_ge(sem["sC%d" % t], 1)
+            dve.wait_ge(sem.zr, 1)
+            dve.tensor_scalar(T["ob%d" % t][:, 1:2 * WIN:2 * QP + 2], T.zer[:, 0:2], T.nb[:, t:t + 1], None, A.add
                               ).then_inc(sem["sB%d" % t], 1)
+
+        def sum_out(t):
+            dve.wait_ge(sem["xE%d0" % t], 1)
+            dve.wait_ge(sem["xE%d1" % t], 1)
+            dve.wait_ge(sem.zr, 1)
+            dve.tensor_scalar(T["ob%d" % t][:, 0:2 * WIN - 1:2 * QP + 2], T.zer[:, 0:2], T.ls[:, 2 * t:2 * t + 1],
+                              T.ls[:, 2 * t + 1:2 * t + 2], A.add, A.add).then_inc(sem["sL%d" % t], 1)
+
+        def own_cols(t):
+            dve.wait_ge(sem["sC%d" % t], 1)
+            dve.tensor_copy(T.land[:, SLOT * slot + kc:SLOT * slot + kc + 1], T.nb[:, t:t + 1]).then_inc(sem.sBo, 1)
+            dve.wait_ge(sem["xE%d0" % t], 1)
+            dve.wait_ge(sem["xE%d1" % t], 1)
+            dve.tensor_tensor(T.land[:, SLOT * slot + lc:SLOT * slot + lc + 1], T.ls[:, 2 * t:2 * t + 1],
+                              T.ls[:, 2 * t + 1:2 * t + 2], A.add).then_inc(sem.sLo, 1)
 
         def expo(t, b):
             act.wait_ge(sem["sC%d" % t], 1)
             act.activation(T["p%d" % t][:, 128 * b:128 * b + 128], T["ps%d" % t][:, 128 * b:128 * b + 128], AF.Exp,
-                           bias=T.nb[:, t:t + 1], scale=1.0).then_inc(sem["xE%d%d" % (t, b)], 1)
+                           bias=T.nb[:, t:t + 1], scale=1.0, accum_out=T.ls[:, 2 * t + b:2 * t + b + 1]
+                           ).then_inc(sem["xE%d%d" % (t, b)], 1)
 
         def turn(t, b):
             pe.wait_ge(sem.idd, 1)
@@ -204,62 +215,95 @@ def rank_program(g, core, T, topo):
             dve.tensor_copy(T["pt%d" % t][:, 128 * b:128 * b + 128], bank[(t, b)][:, 0:128]
                             ).then_inc(sem["xP%d%d" % (t, b)], 1)
 
-        def PV(t, b):
+        def VP(t, b):
             pe.wait_ge(sem["xP%d%d" % (t, b)], 1)
             pe.wait_ge(sem.vs, v_ready)
-            if is_mem:
-                pe.wait_ge(sem.vone, 2)
-            i = pe.matmul(T["ps%d" % t][:, 256:385], T["pt%d" % t][:, 128 * b:128 * b + 128],
-                          T.vbuf[:, SLOT * b:SLOT * b + 129], b == 0, b == 1)
+            lo, n = (0, 128) if t != LAST else (QP * hp, QP)
+            i = pe.matmul(T["ps%d" % t][:, 256:256 + n], T.vbuf[:, 128 * b:128 * b + 128],
+                          T["pt%d" % t][:, 128 * b + lo:128 * b + lo + n], b == 0, b == 1)
             if b == 1:
                 i.then_inc(sem["sO%d" % t], 1)
 
+        def PV_own(b):
+            if b == 0:
+                pe.wait_ge(sem["sR%d" % o0], 1)
+            i = pe.matmul(turned_bank[slot][:, 0:128], T["pt%d" % LAST][:, 128 * b:128 * b + 128],
+                          T.vbuf[:, 128 * b:128 * b + 128], b == 0, b == 1)
+            if b == 1:
+                i.then_inc(sem["tT%d" % slot], 1)
+
         def out(t):
             act.wait_ge(sem["sO%d" % t], 1)
-            act.activation(res_cols(t, 0, 129), T["ps%d" % t][:, 256:385], AF.Copy).then_inc(sem["sR%d" % t], 1)
+            lo, n = (0, 128) if t != LAST else (QP * hp, QP)
+            act.activation(T["ob%d" % t][:, 2 + lo:2 + lo + n], T["ps%d" % t][:, 256:256 + n], AF.Copy
+                           ).then_inc(sem["sR%d" % t], 1)
 
         S(o0); S(o1); S(o2); turn(o0, 0); turn(o0, 1); turn(o1, 0); turn(o1, 1)
-        PV(o0, 0); PV(o0, 1); PV(o1, 0); PV(o1, 1); turn(o2, 0); turn(o2, 1); PV(o2, 0); PV(o2, 1)
-        top(o0); whole(o0); bias(o0); top(o1); whole(o1); bias(o1); turned(o0, 0); turned(o0, 1); step_out(o0)
-        top(o2); turned(o1, 0); whole(o2); turned(o1, 1); bias(o2); step_out(o1); step_out(o2)
-        turned(o2, 0); turned(o2, 1)
+        VP(o0, 0); VP(o0, 1); VP(o1, 0); VP(o1, 1); turn(o2, 0); turn(o2, 1); VP(o2, 0); VP(o2, 1)
+        PV_own(0); PV_own(1)
+        pe.wait_ge(sem["sR%d" % o1], 1)
+        top(o0); top(o1); top(o2); turned(o0, 0); turned(o0, 1); step_out(o0); sum_out(o0)
+        turned(o1, 0); turned(o1, 1); step_out(o1); sum_out(o1); step_out(o2)
+        turned(o2, 0); sum_out(o2); own_cols(o2); turned(o2, 1)
         expo(o0, 0); expo(o0, 1); expo(o1, 0); expo(o1, 1); out(o0); expo(o2, 0); expo(o2, 1); out(o1); out(o2)
 
         for t in order:
             g.wait_ge(sem["sR%d" % t], 1)
             g.wait_ge(sem["sB%d" % t], 1)
-            dsts = [c for c in mine[2 * t:2 * t + 2] if c != core]
-            send(T.land[:, SLOT * slot:SLOT * slot + USED], res_cols(t, 0, USED), dsts, sem["pa%d" % slot], NR)
-
-    dve, act = g.vector, g.scalar
-    for q_ in (dve, act):
-        for s in range(2):
-            if s == slot:
-                q_.wait_ge(sem["sR%d" % tile], 1)
-                q_.wait_ge(sem["sB%d" % tile], 1)
+            g.wait_ge(sem["sL%d" % t], 1)
+            parts = [(lands(slot, h), T["ob%d" % t][:, WIN * h:WIN * h + WIN], c)
+                     for h, c in enumerate(mine[2 * t:2 * t + 2]) if c != core]
+            if len(parts) == 1:
+                send(parts[0][0], parts[0][1], parts[0][2], sem["pa%d" % slot], NR)
             else:
-                q_.wait_ge(sem["pa%d" % s], NR)
-    steps = T.land[:, 129:SLOT + 130:SLOT]
-    dve.tensor_scalar(T.km1[:, 0:1], T.land[:, 129:130], T.land[:, SLOT + 129:SLOT + 130], 1.0, A.max, A.subtract
+                send_each(parts, sem["pa%d" % slot], NR)
+
+    arrives = NR if tile == LAST else NR // 2
+    p0 = QP * half
+    for s in others:
+        pe.wait_ge(sem["pa%d" % s], arrives)
+        pe.wait_ge(sem.idd, 1)
+        if half == 0:
+            pe.matmul(turned_bank[s][0:QP, 0:128], T.land[:, SLOT * s + 2:SLOT * s + 2 + QP], T.ident[:], True, True
+                      ).then_inc(sem["tT%d" % s], 1)
+        else:
+            pe.wait_ge(sem.lz, len(others))
+            pe.matmul(turned_bank[s][:, 0:128], T.land[:, SLOT * s:SLOT * s + 128], T.ident[:], True, True
+                      ).then_inc(sem["tT%d" % s], 1)
+
+    def rows(buf, a, b, step=1):
+        return buf[p0:p0 + QP, a:b:step]
+
+    for s in range(2):
+        if s == slot:
+            dve.wait_ge(sem.sBo, 1)
+            dve.wait_ge(sem.sLo, 1)
+        else:
+            dve.wait_ge(sem["pa%d" % s], arrives)
+    negs = rows(T.land, kc, SLOT + kc + 1, SLOT)
+    sums = rows(T.land, lc, SLOT + lc + 1, SLOT)
+    dve.tensor_tensor(rows(T.nm, 0, 1), rows(T.land, kc, kc + 1), rows(T.land, SLOT + kc, SLOT + kc + 1), A.min
                       ).then_inc(sem.m1, 1)
-    dve.wait_ge(sem.m1, 1)
-    dve.tensor_scalar(T.xx[:, 0:2], steps, T.km1[:, 0:1], -1.0, A.subtract, A.max).then_inc(sem.m2, 1)
-    dve.wait_ge(sem.m2, 1)
-    dve.tensor_scalar(T.ww[:, 0:2], T.xx[:, 0:2], 1.0, EPS, A.add, A.mult).then_inc(sem.m3, 1)
-    dve.wait_ge(sem.m3, 1)
-    dve.tensor_tensor(T.ab[:, 0:2], T.xx[:, 0:2], T.ww[:, 0:2], A.max).then_inc(sem.m4, 1)
-    dve.wait_ge(sem.m4, 1)
+    act.wait_ge(sem.m1, 1)
+    act.activation(rows(T.ab, 0, 2), negs, AF.Exp, bias=rows(T.nm, 0, 1), scale=-1.0).then_inc(sem.m4, 1)
     act.wait_ge(sem.m4, 1)
-    dve.tensor_scalar(T.ta[:, 0:129], T.land[:, 0:129], T.ab[:, 0:1], None, A.mult).then_inc(sem.m5, 1)
-    act.activation(T.psm[:, 0:129], T.land[:, SLOT:SLOT + 129], AF.Copy, scale=T.ab[:, 1:2]).then_inc(sem.m6, 1)
+    act.wait_ge(sem.tT0, 1)
+    act.activation(rows(T.ta, 0, 128), rows(turned_bank[0], 0, 128), AF.Copy, scale=rows(T.ab, 0, 1)).then_inc(sem.mA, 1)
+    act.wait_ge(sem.tT1, 1)
+    act.activation(rows(T.psm, 0, 128), rows(turned_bank[1], 0, 128), AF.Copy, scale=rows(T.ab, 1, 2)).then_inc(sem.mB, 1)
+    dve.wait_ge(sem.m4, 1)
+    dve.tensor_tensor(rows(T.lw, 0, 2), sums, rows(T.ab, 0, 2), A.mult).then_inc(sem.m5, 1)
     dve.wait_ge(sem.m5, 1)
+    dve.tensor_tensor(rows(T.lt, 0, 1), rows(T.lw, 0, 1), rows(T.lw, 1, 2), A.add).then_inc(sem.m6, 1)
     dve.wait_ge(sem.m6, 1)
-    dve.tensor_tensor(T.tt[:, 0:129], T.ta[:, 0:129], T.psm[:, 0:129], A.add).then_inc(sem.m7, 1)
+    dve.reciprocal(rows(T.rr, 0, 1), rows(T.lt, 0, 1)).then_inc(sem.m7, 1)
+    dve.wait_ge(sem.mA, 1)
+    dve.wait_ge(sem.mB, 1)
+    dve.tensor_tensor(rows(T.tt, 0, 128), rows(T.ta, 0, 128), rows(T.psm, 0, 128), A.add).then_inc(sem.m8, 1)
     dve.wait_ge(sem.m7, 1)
-    dve.reciprocal(T.rr[:, 0:1], T.tt[:, 128:129]).then_inc(sem.m8, 1)
     dve.wait_ge(sem.m8, 1)
-    dve.tensor_scalar(T.ybuf[:], T.tt[:, 0:128], T.rr[:, 0:1], None, A.mult).then_inc(sem.m9, 1)
+    dve.tensor_scalar(rows(T.ybuf, 0, 128), rows(T.tt, 0, 128), rows(T.rr, 0, 1), None, A.mult).then_inc(sem.m9, 1)
     g.sync.wait_ge(sem.m9, 1)
-    g.sync.dma_start(T.y[:], T.ybuf[QP * half:QP * half + QP, :]).then_inc(sem.st, 16)
+    g.sync.dma_start(T.y[:], T.ybuf[p0:p0 + QP, :]).then_inc(sem.st, 16)
     g.sync.wait_ge(sem.st, 16)
     g.wait_ge(sem.loc, sent[0])

@@ -7,10 +7,16 @@ LAST = NT - 1
 KEYS = 256
 SLOT = 136
 WIN = QP + 2
+PAD = 8
+CAP = 30.0
+CAP2 = 20.0
 NQ, NK, NR = 8, 8, 8
 
 SCRATCH = {
-    "qall": ("sbuf", [128, 2 * NT * QP], "bfloat16"),
+    "qall": ("sbuf", [128, 2 * NT * QP + PAD], "bfloat16"),
+    "pown": ("sbuf", [128, KEYS], "bfloat16"),
+    "ptown": ("sbuf", [128, 2 * QP], "bfloat16"),
+    "lr": ("sbuf", [128, 4], "float32"),
     "kbuf": ("sbuf", [128, KEYS], "bfloat16"),
     "vbuf": ("sbuf", [128, KEYS], "bfloat16"),
     "zer": ("sbuf", [128, 128], "bfloat16"),
@@ -21,9 +27,9 @@ SCRATCH = {
     "ls": ("sbuf", [128, 8], "float32"),
     "nm": ("sbuf", [128, 4], "float32"),
     "ab": ("sbuf", [128, 4], "float32"),
-    "lw": ("sbuf", [128, 4], "float32"),
     "lt": ("sbuf", [128, 4], "float32"),
     "ta": ("sbuf", [128, 128], "float32"),
+    "tab": ("sbuf", [128, 128], "bfloat16"),
     "tt": ("sbuf", [128, 128], "float32"),
     "rr": ("sbuf", [128, 4], "float32"),
     "ybuf": ("sbuf", [128, 128], "bfloat16"),
@@ -38,7 +44,8 @@ for _t in range(4):
     SCRATCH["pst%d" % _t] = ("psum", [128, 1024], "bfloat16")
 
 SEMAPHORES = ["zr", "qld", "ks", "vs", "idn", "idd", "pa0", "pa1", "loc", "st", "lz", "sLo", "sBo", "tT0", "tT1",
-              "m1", "m4", "m5", "m6", "m7", "m8", "m9", "mA", "mB"]
+              "m1", "m4", "m6", "m7", "m8", "m9", "mA", "eS", "eC", "eE", "eL", "eZ", "eT0", "eT1", "eP0", "eP1",
+              "sA", "r1", "r2"]
 for _t in range(NT):
     SEMAPHORES += ["%s%d" % (_n, _t) for _n in ("qa", "sS", "sC", "sB", "sL", "sO", "sR")]
     SEMAPHORES += ["%s%d%d" % (_n, _t, _b) for _n in ("xE", "xT", "xP") for _b in range(2)]
@@ -75,7 +82,7 @@ def rank_program(g, core, T, topo):
     mem, members, server, rack_of = _plan(T, topo)
     R = rack_of(core)
     srv = [server[(R, s)] for s in range(len(mem))]
-    mine = [c for c in members[R] if c not in srv] + srv
+    mine = [c for c in members[R] if c not in srv] + sorted(srv, key=lambda c: c not in mem)
     idx = mine.index(core)
     tile, half = idx // 2, idx % 2
     slot = srv.index(core) if core in srv else None
@@ -117,20 +124,31 @@ def rank_program(g, core, T, topo):
     def lands(s, h):
         return T.land[:, SLOT * s:SLOT * s + WIN] if h == 0 else T.land[:, SLOT * s + QP:SLOT * s + QP + WIN]
 
-    myq = T.qall[:, QP * idx:QP * idx + QP]
+    def tcol(t):
+        return 128 * t + (PAD if t == LAST else 0)
+
+    q0 = tcol(tile) + QP * half
+    myq = T.qall[:, q0:q0 + QP]
+    LA, NA = tcol(LAST) - 2, tcol(LAST) - 1
     lc = 0 if half == 0 else 2 * QP
     kc = lc + 1
     others = [s for s in range(2) if s != slot]
 
     if is_mem:
         g.sync.dma_start(T.kbuf[:], T.k[:]).then_inc(sem.ks, 16)
-        g.scalar.dma_start(myq, T.q[:]).then_inc(sem.qld, 16)
+        g.sync.dma_start(myq, T.q[:]).then_inc(sem.qld, 16)
         g.sync.dma_start(T.vbuf[:], T.v[:]).then_inc(sem.vs, 16)
     else:
         g.sync.dma_start(myq, T.q[:]).then_inc(sem.qld, 16)
     dve.memset(T.zer[:], 0.0).then_inc(sem.zr, 1)
     act.wait_ge(sem.zr, 1)
-    act.activation(T.ones[:], T.zer[:], AF.Exp).then_inc(sem.idn, 1)
+    if is_mem:
+        dve.memset(T.ones[:], 1.0).then_inc(sem.idn, 1)
+        act.activation(T.qall[QP:128, LA:NA + 1], T.zer[QP:128, 0:2], AF.Exp).then_inc(sem.eZ, 1)
+        g.wait_ge(sem.idn, 1)
+        g.affine_select(T.ident[:], T.ones[:], [[-1, 128]], A.is_equal, 0.0, 0, 1).then_inc(sem.idd, 1)
+    else:
+        act.activation(T.ones[:], T.zer[:], AF.Exp).then_inc(sem.idn, 1)
     if half == 1:
         for s in others:
             dve.memset(T.land[:, SLOT * s:SLOT * s + QP], 0.0).then_inc(sem.lz, 1)
@@ -143,14 +161,20 @@ def rank_program(g, core, T, topo):
             send(T.kbuf[:], T.kbuf[:], d, sem.ks, NK)
     targets = sorted([d for d in srv if d != core], key=lambda d: tile_order(d).index(tile))
     g.wait_ge(sem.qld, 16)
+    if is_mem:
+        g.wait_ge(sem.eC, 1)
+        g.wait_ge(sem.eL, 1)
+        g.wait_ge(sem.eZ, 1)
+    qsent = T.qall[:, LA:q0 + QP] if is_mem else myq
     for d in targets:
-        send(myq, myq, d, sem["qa%d" % tile], NQ)
+        send(qsent, qsent, d, sem["qa%d" % tile], NQ)
     if is_mem:
         g.wait_ge(sem.vs, 16)
         for d in copies:
             send(T.vbuf[:], T.vbuf[:], d, sem.vs, NK)
-    g.wait_ge(sem.idn, 1)
-    g.affine_select(T.ident[:], T.ones[:], [[-1, 128]], A.is_equal, 0.0, 0, 1).then_inc(sem.idd, 1)
+    if not is_mem:
+        g.wait_ge(sem.idn, 1)
+        g.affine_select(T.ident[:], T.ones[:], [[-1, 128]], A.is_equal, 0.0, 0, 1).then_inc(sem.idd, 1)
 
     turned_bank = {0: T.ps0, 1: T.ps1}
 
@@ -169,7 +193,7 @@ def rank_program(g, core, T, topo):
                     pe.wait_ge(sem.qld, 16)
             pe.wait_ge(sem["qa%d" % t], NQ * len([c for c in mine[2 * t:2 * t + 2] if c != core]))
             pe.wait_ge(sem.ks, k_ready)
-            pe.matmul(T["ps%d" % t][:, 0:KEYS], T.qall[:, 128 * t:128 * t + 128], T.kbuf[:], True, True
+            pe.matmul(T["ps%d" % t][:, 0:KEYS], T.qall[:, tcol(t):tcol(t) + 128], T.kbuf[:], True, True
                       ).then_inc(sem["sS%d" % t], 1)
 
         def top(t):
@@ -177,8 +201,27 @@ def rank_program(g, core, T, topo):
             dve.tensor_reduce(T.nb[:, t:t + 1], T["ps%d" % t][:, 0:KEYS], AxisListType.X, A.max, negate=True
                               ).then_inc(sem["sC%d" % t], 1)
 
-        def step_out(t):
+        def fixed(t):
+            return sem.sA if (t == LAST and not is_mem) else sem["sC%d" % t]
+
+        def adopt(t):
             dve.wait_ge(sem["sC%d" % t], 1)
+            dve.wait_ge(sem["qa%d" % t], NQ)
+            dve.tensor_scalar(T.nb[0:QP, t:t + 1], T.nb[0:QP, t:t + 1], CAP, T.qall[0:QP, NA:NA + 1], A.add, A.min
+                              ).then_inc(sem.sA, 1)
+
+        def ratio_out(t):
+            dve.wait_ge(sem["xE%d0" % t], 1)
+            dve.wait_ge(sem["xE%d1" % t], 1)
+            dve.tensor_scalar(T.lr[0:QP, 0:1], T.qall[0:QP, LA:LA + 1], T.ls[0:QP, 2 * t:2 * t + 1],
+                              T.ls[0:QP, 2 * t + 1:2 * t + 2], A.add, A.add).then_inc(sem.r1, 1)
+            dve.wait_ge(sem.r1, 1)
+            dve.reciprocal(T.lr[0:QP, 1:2], T.lr[0:QP, 0:1]).then_inc(sem.r2, 1)
+            dve.wait_ge(sem.r2, 1)
+            dve.tensor_copy(T["ob%d" % t][0:QP, 0:1], T.lr[0:QP, 1:2]).then_inc(sem["sL%d" % t], 1)
+
+        def step_out(t):
+            dve.wait_ge(fixed(t), 1)
             dve.wait_ge(sem.zr, 1)
             dve.tensor_scalar(T["ob%d" % t][:, 1:2 * WIN:2 * QP + 2], T.zer[:, 0:2], T.nb[:, t:t + 1], None, A.add
                               ).then_inc(sem["sB%d" % t], 1)
@@ -191,7 +234,7 @@ def rank_program(g, core, T, topo):
                               T.ls[:, 2 * t + 1:2 * t + 2], A.add, A.add).then_inc(sem["sL%d" % t], 1)
 
         def own_cols(t):
-            dve.wait_ge(sem["sC%d" % t], 1)
+            dve.wait_ge(fixed(t), 1)
             dve.tensor_copy(T.land[:, SLOT * slot + kc:SLOT * slot + kc + 1], T.nb[:, t:t + 1]).then_inc(sem.sBo, 1)
             dve.wait_ge(sem["xE%d0" % t], 1)
             dve.wait_ge(sem["xE%d1" % t], 1)
@@ -199,7 +242,7 @@ def rank_program(g, core, T, topo):
                               T.ls[:, 2 * t + 1:2 * t + 2], A.add).then_inc(sem.sLo, 1)
 
         def expo(t, b):
-            act.wait_ge(sem["sC%d" % t], 1)
+            act.wait_ge(fixed(t), 1)
             act.activation(T["p%d" % t][:, 128 * b:128 * b + 128], T["ps%d" % t][:, 128 * b:128 * b + 128], AF.Exp,
                            bias=T.nb[:, t:t + 1], scale=1.0, accum_out=T.ls[:, 2 * t + b:2 * t + b + 1]
                            ).then_inc(sem["xE%d%d" % (t, b)], 1)
@@ -207,6 +250,8 @@ def rank_program(g, core, T, topo):
         def turn(t, b):
             pe.wait_ge(sem.idd, 1)
             pe.wait_ge(sem["xE%d%d" % (t, b)], 1)
+            if t == o2:
+                pe.wait_ge(sem["xP%d%d" % (o0, b)], 1)
             pe.transpose(bank[(t, b)][:, 0:128], T["p%d" % t][:, 128 * b:128 * b + 128], T.ident[:]
                          ).then_inc(sem["xT%d%d" % (t, b)], 1)
 
@@ -238,19 +283,61 @@ def rank_program(g, core, T, topo):
             act.activation(T["ob%d" % t][:, 2 + lo:2 + lo + n], T["ps%d" % t][:, 256:256 + n], AF.Copy
                            ).then_inc(sem["sR%d" % t], 1)
 
-        S(o0); S(o1); S(o2); turn(o0, 0); turn(o0, 1); turn(o1, 0); turn(o1, 1)
-        VP(o0, 0); VP(o0, 1); VP(o1, 0); VP(o1, 1); turn(o2, 0); turn(o2, 1); VP(o2, 0); VP(o2, 1)
-        PV_own(0); PV_own(1)
-        pe.wait_ge(sem["sR%d" % o1], 1)
-        top(o0); top(o1); top(o2); turned(o0, 0); turned(o0, 1); step_out(o0); sum_out(o0)
-        turned(o1, 0); turned(o1, 1); step_out(o1); sum_out(o1); step_out(o2)
-        turned(o2, 0); sum_out(o2); own_cols(o2); turned(o2, 1)
-        expo(o0, 0); expo(o0, 1); expo(o1, 0); expo(o1, 1); out(o0); expo(o2, 0); expo(o2, 1); out(o1); out(o2)
+        def out_v(t):
+            dve.wait_ge(sem["sO%d" % t], 1)
+            dve.tensor_copy(T["ob%d" % t][:, 2:2 + 128], T["ps%d" % t][:, 256:256 + 128]).then_inc(sem["sR%d" % t], 1)
+
+        if is_mem:
+            se = T.psm[0:QP, 256:256 + KEYS]
+            pe.wait_ge(sem.ks, 16)
+            pe.wait_ge(sem.qld, 16)
+            pe.matmul(se, myq, T.kbuf[:], True, True).then_inc(sem.eS, 1)
+            dve.wait_ge(sem.eS, 1)
+            dve.tensor_reduce(T.qall[0:QP, NA:NA + 1], se, AxisListType.X, A.max, negate=True).then_inc(sem.eC, 1)
+            act.wait_ge(sem.eC, 1)
+            act.activation(T.pown[0:QP, :], se, AF.Exp, bias=T.qall[0:QP, NA:NA + 1], scale=1.0,
+                           accum_out=T.ls[0:QP, 6:7]).then_inc(sem.eE, 1)
+            dve.wait_ge(sem.eE, 1)
+            dve.tensor_copy(T.qall[0:QP, LA:LA + 1], T.ls[0:QP, 6:7]).then_inc(sem.eL, 1)
+            pe.wait_ge(sem.idd, 1)
+            pe.wait_ge(sem.eE, 1)
+            for b_ in range(2):
+                pe.transpose(bank[(o1, b_)][:, 0:QP], T.pown[0:QP, 128 * b_:128 * b_ + 128], T.ident[0:QP, 0:QP]
+                             ).then_inc(sem["eT%d" % b_], 1)
+            for b_ in range(2):
+                dve.wait_ge(sem["eT%d" % b_], 1)
+                dve.tensor_copy(T.ptown[:, QP * b_:QP * b_ + QP], bank[(o1, b_)][:, 0:QP]).then_inc(sem["eP%d" % b_], 1)
+            pe.wait_ge(sem.eP0, 1)
+            pe.wait_ge(sem.eP1, 1)
+            pe.wait_ge(sem.vs, 16)
+            for b_ in range(2):
+                pe.matmul(T.psm[0:QP, 0:128], T.ptown[:, QP * b_:QP * b_ + QP], T.vbuf[:, 128 * b_:128 * b_ + 128],
+                          b_ == 0, False)
+        else:
+            dve.memset(T["ob%d" % LAST][QP:128, 0:1], 0.0).then_inc(sem["sL%d" % LAST], 1)
+
+        S(o0); S(o1); S(o2); turn(o0, 0); turn(o0, 1); turn(o1, 0); turn(o1, 1); turn(o2, 0); turn(o2, 1)
+        VP(o0, 0); VP(o0, 1); VP(o1, 0); VP(o1, 1); VP(o2, 0); VP(o2, 1)
+        if not is_mem:
+            PV_own(0); PV_own(1)
+            pe.wait_ge(sem["sR%d" % o1], 1)
+        top(o0); top(o1); top(o2)
+        if not is_mem:
+            adopt(o2)
+        turned(o0, 0); turned(o0, 1); step_out(o0); sum_out(o0)
+        turned(o1, 0); turned(o1, 1); step_out(o1); sum_out(o1)
+        turned(o2, 0); turned(o2, 1); step_out(o2)
+        if is_mem:
+            sum_out(o2)
+        else:
+            ratio_out(o2); own_cols(o2)
+        out_v(o1)
+        expo(o0, 0); expo(o0, 1); expo(o1, 0); expo(o1, 1); expo(o2, 0); expo(o2, 1); out(o0); out(o2)
 
         for t in order:
             g.wait_ge(sem["sR%d" % t], 1)
             g.wait_ge(sem["sB%d" % t], 1)
-            g.wait_ge(sem["sL%d" % t], 1)
+            g.wait_ge(sem["sL%d" % t], 2 if (t == LAST and not is_mem) else 1)
             parts = [(lands(slot, h), T["ob%d" % t][:, WIN * h:WIN * h + WIN], c)
                      for h, c in enumerate(mine[2 * t:2 * t + 2]) if c != core]
             if len(parts) == 1:
@@ -260,49 +347,74 @@ def rank_program(g, core, T, topo):
 
     arrives = NR if tile == LAST else NR // 2
     p0 = QP * half
-    for s in others:
-        pe.wait_ge(sem["pa%d" % s], arrives)
-        pe.wait_ge(sem.idd, 1)
-        if half == 0:
-            pe.matmul(turned_bank[s][0:QP, 0:128], T.land[:, SLOT * s + 2:SLOT * s + 2 + QP], T.ident[:], True, True
-                      ).then_inc(sem["tT%d" % s], 1)
-        else:
-            pe.wait_ge(sem.lz, len(others))
-            pe.matmul(turned_bank[s][:, 0:128], T.land[:, SLOT * s:SLOT * s + 128], T.ident[:], True, True
-                      ).then_inc(sem["tT%d" % s], 1)
 
     def rows(buf, a, b, step=1):
         return buf[p0:p0 + QP, a:b:step]
 
-    for s in range(2):
-        if s == slot:
-            dve.wait_ge(sem.sBo, 1)
-            dve.wait_ge(sem.sLo, 1)
+    if is_mem:
+        s = others[0]
+        pe.wait_ge(sem["pa%d" % s], arrives)
+        pe.matmul(T.psm[0:QP, 0:128], T.land[:, SLOT * s + 2:SLOT * s + 2 + QP], T.ident[:], False, True
+                  ).then_inc(sem["tT%d" % s], 1)
+        dve.wait_ge(sem["pa%d" % s], arrives)
+        dve.wait_ge(sem["tT%d" % s], 1)
+        dve.tensor_scalar(T.ybuf[0:QP, :], T.psm[0:QP, 0:128], T.land[0:QP, SLOT * s:SLOT * s + 1], None, A.mult
+                          ).then_inc(sem.m9, 1)
+    else:
+        plain = slot is None
+        np_ = QP if half == 0 else 128
+
+        def wide(buf, a, b):
+            return buf[0:np_, a:b] if plain else rows(buf, a, b)
+
+        for s in others:
+            pe.wait_ge(sem["pa%d" % s], arrives)
+            pe.wait_ge(sem.idd, 1)
+            opened = plain and s == 0
+            if half == 0:
+                i = pe.matmul(turned_bank[s][0:QP, 0:128], T.land[:, SLOT * s + 2:SLOT * s + 2 + QP], T.ident[:],
+                              True, not opened)
+            else:
+                pe.wait_ge(sem.lz, len(others))
+                i = pe.matmul(turned_bank[s][:, 0:128], T.land[:, SLOT * s:SLOT * s + 128], T.ident[:], True, not opened)
+            if not opened:
+                i.then_inc(sem["tT%d" % s], 1)
+        for s in range(2):
+            if s == slot:
+                dve.wait_ge(sem.sBo, 1)
+                dve.wait_ge(sem.sLo, 1)
+            else:
+                dve.wait_ge(sem["pa%d" % s], arrives)
+        dve.tensor_scalar(wide(T.nm, 0, 1), wide(T.land, kc, kc + 1), wide(T.land, SLOT + kc, SLOT + kc + 1), CAP2,
+                          A.subtract, A.min).then_inc(sem.m1, 1)
+        act.wait_ge(sem.m1, 1)
+        act.activation(wide(T.ab, 0, 1), wide(T.nm, 0, 1), AF.Exp).then_inc(sem.m4, 1)
+        act.wait_ge(sem.m4, 1)
+        act.wait_ge(sem.tT1, 1)
+        act.activation(wide(T.tab if plain else T.ta, 0, 128), wide(turned_bank[1], 0, 128), AF.Copy,
+                       scale=wide(T.ab, 0, 1)).then_inc(sem.mA, 1)
+        dve.wait_ge(sem.m4, 1)
+        dve.tensor_scalar(rows(T.lt, 0, 1), rows(T.ab, 0, 1), rows(T.land, SLOT + lc, SLOT + lc + 1),
+                          rows(T.land, lc, lc + 1), A.mult, A.add).then_inc(sem.m6, 1)
+        dve.wait_ge(sem.m6, 1)
+        dve.reciprocal(rows(T.rr, 0, 1), rows(T.lt, 0, 1)).then_inc(sem.m7, 1)
+        if plain:
+            pe.wait_ge(sem.mA, 1)
+            pe.matmul(turned_bank[0][0:np_, 0:128], T.ident[0:np_, 0:np_], T.tab[0:np_, 0:128], False, True
+                      ).then_inc(sem.tT0, 1)
+            dve.wait_ge(sem.tT0, 1)
+            dve.wait_ge(sem.m7, 1)
+            dve.tensor_scalar(rows(T.ybuf, 0, 128), rows(turned_bank[0], 0, 128), rows(T.rr, 0, 1), None, A.mult
+                              ).then_inc(sem.m9, 1)
         else:
-            dve.wait_ge(sem["pa%d" % s], arrives)
-    negs = rows(T.land, kc, SLOT + kc + 1, SLOT)
-    sums = rows(T.land, lc, SLOT + lc + 1, SLOT)
-    dve.tensor_tensor(rows(T.nm, 0, 1), rows(T.land, kc, kc + 1), rows(T.land, SLOT + kc, SLOT + kc + 1), A.min
-                      ).then_inc(sem.m1, 1)
-    act.wait_ge(sem.m1, 1)
-    act.activation(rows(T.ab, 0, 2), negs, AF.Exp, bias=rows(T.nm, 0, 1), scale=-1.0).then_inc(sem.m4, 1)
-    act.wait_ge(sem.m4, 1)
-    act.wait_ge(sem.tT0, 1)
-    act.activation(rows(T.ta, 0, 128), rows(turned_bank[0], 0, 128), AF.Copy, scale=rows(T.ab, 0, 1)).then_inc(sem.mA, 1)
-    act.wait_ge(sem.tT1, 1)
-    act.activation(rows(T.psm, 0, 128), rows(turned_bank[1], 0, 128), AF.Copy, scale=rows(T.ab, 1, 2)).then_inc(sem.mB, 1)
-    dve.wait_ge(sem.m4, 1)
-    dve.tensor_tensor(rows(T.lw, 0, 2), sums, rows(T.ab, 0, 2), A.mult).then_inc(sem.m5, 1)
-    dve.wait_ge(sem.m5, 1)
-    dve.tensor_tensor(rows(T.lt, 0, 1), rows(T.lw, 0, 1), rows(T.lw, 1, 2), A.add).then_inc(sem.m6, 1)
-    dve.wait_ge(sem.m6, 1)
-    dve.reciprocal(rows(T.rr, 0, 1), rows(T.lt, 0, 1)).then_inc(sem.m7, 1)
-    dve.wait_ge(sem.mA, 1)
-    dve.wait_ge(sem.mB, 1)
-    dve.tensor_tensor(rows(T.tt, 0, 128), rows(T.ta, 0, 128), rows(T.psm, 0, 128), A.add).then_inc(sem.m8, 1)
-    dve.wait_ge(sem.m7, 1)
-    dve.wait_ge(sem.m8, 1)
-    dve.tensor_scalar(rows(T.ybuf, 0, 128), rows(T.tt, 0, 128), rows(T.rr, 0, 1), None, A.mult).then_inc(sem.m9, 1)
+            dve.wait_ge(sem.mA, 1)
+            dve.wait_ge(sem.tT0, 1)
+            dve.tensor_tensor(rows(T.tt, 0, 128), rows(turned_bank[0], 0, 128), rows(T.ta, 0, 128), A.add
+                              ).then_inc(sem.m8, 1)
+            dve.wait_ge(sem.m7, 1)
+            dve.wait_ge(sem.m8, 1)
+            dve.tensor_scalar(rows(T.ybuf, 0, 128), rows(T.tt, 0, 128), rows(T.rr, 0, 1), None, A.mult
+                              ).then_inc(sem.m9, 1)
     g.sync.wait_ge(sem.m9, 1)
     g.sync.dma_start(T.y[:], T.ybuf[p0:p0 + QP, :]).then_inc(sem.st, 16)
     g.sync.wait_ge(sem.st, 16)

from concourse.bass import DstId, RemoteDMATransfer
from concourse.mybir import AluOpType, AxisListType, ActivationFunctionType

QP = 64
NT = 3
LAST = NT - 1
KEYS = 256
SLOT = 136
WIN = QP + 2
PAD = 8
CAP = 30.0
CAP2 = 20.0
NQ, NK, NR = 8, 8, 8

SCRATCH = {
    "qall": ("sbuf", [128, 2 * NT * QP + PAD], "bfloat16"),
    "pown": ("sbuf", [128, KEYS], "bfloat16"),
    "ptown": ("sbuf", [128, 2 * QP], "bfloat16"),
    "lr": ("sbuf", [128, 4], "float32"),
    "kbuf": ("sbuf", [128, KEYS], "bfloat16"),
    "vbuf": ("sbuf", [128, KEYS], "bfloat16"),
    "zer": ("sbuf", [128, 128], "bfloat16"),
    "ones": ("sbuf", [128, 128], "bfloat16"),
    "ident": ("sbuf", [128, 128], "bfloat16"),
    "land": ("sbuf", [128, 2 * SLOT], "bfloat16"),
    "nb": ("sbuf", [128, 8], "bfloat16"),
    "ls": ("sbuf", [128, 8], "float32"),
    "nm": ("sbuf", [128, 4], "float32"),
    "ab": ("sbuf", [128, 4], "float32"),
    "lt": ("sbuf", [128, 4], "float32"),
    "ta": ("sbuf", [128, 128], "float32"),
    "tab": ("sbuf", [128, 128], "bfloat16"),
    "tt": ("sbuf", [128, 128], "float32"),
    "rr": ("sbuf", [128, 4], "float32"),
    "ybuf": ("sbuf", [128, 128], "bfloat16"),
    "psm": ("psum", [128, 512], "float32"),
}
for _t in range(NT):
    SCRATCH["p%d" % _t] = ("sbuf", [128, KEYS], "bfloat16")
    SCRATCH["pt%d" % _t] = ("sbuf", [128, KEYS], "bfloat16")
    SCRATCH["ob%d" % _t] = ("sbuf", [128, SLOT], "bfloat16")
    SCRATCH["ps%d" % _t] = ("psum", [128, 512], "float32")
for _t in range(4):
    SCRATCH["pst%d" % _t] = ("psum", [128, 1024], "bfloat16")

SEMAPHORES = ["zr", "qld", "ks", "vs", "idn", "idd", "pa0", "pa1", "loc", "st", "lz", "sLo", "sBo", "tT0", "tT1",
              "m1", "m4", "m6", "m7", "m8", "m9", "mA", "eS", "eC", "eE", "eL", "eZ", "eT0", "eT1", "eP0", "eP1",
              "sA", "r1", "r2"]
for _t in range(NT):
    SEMAPHORES += ["%s%d" % (_n, _t) for _n in ("qa", "sS", "sC", "sB", "sL", "sO", "sR")]
    SEMAPHORES += ["%s%d%d" % (_n, _t, _b) for _n in ("xE", "xT", "xP") for _b in range(2)]


def _plan(T, topo):
    cores = list(T.cores)
    mem = [cores[j] for j in T.tables["MEM"]]

    def rack_of(c):
        return topo.rack(topo.host(c))

    members = {}
    for c in cores:
        members.setdefault(rack_of(c), []).append(c)
    server = {}
    for R in members:
        for s, cj in enumerate(mem):
            if rack_of(cj) == R:
                server[(R, s)] = cj
    for R in members:
        for s, cj in enumerate(mem):
            if (R, s) not in server:
                taken = [server[key] for key in server if key[0] == R]
                server[(R, s)] = [c for c in members[R] if c not in taken and topo.may_write(cj, c)
                                  and topo.chip(c) == topo.chip(cj)][0]
    return mem, members, server, rack_of


def rank_program(g, core, T, topo):
    if T.rank_of(core) is None:
        return
    A, AF = AluOpType, ActivationFunctionType
    mem, members, server, rack_of = _plan(T, topo)
    R = rack_of(core)
    srv = [server[(R, s)] for s in range(len(mem))]
    mine = [c for c in members[R] if c not in srv] + sorted(srv, key=lambda c: c not in mem)
    idx = mine.index(core)
    tile, half = idx // 2, idx % 2
    slot = srv.index(core) if core in srv else None
    is_mem = core in mem
    sem = T.sem
    sent = [0]
    pe, dve, act = g.tensor, g.vector, g.scalar

    def engines(dsts):
        m = topo.mask(core, dsts[0])
        for d in dsts:
            m &= topo.mask(core, d)
        return [e for e in range(16) if (m >> e) & 1]

    def bits(es):
        return sum(1 << e for e in es)

    def send(out_ap, in_ap, d, remote_sem, n):
        rid, pid = topo.addr(d, core)
        g.remote_dma(out_ap, in_ap, remote_sem, sem.loc, pid, rid, bits(engines([d])[:n]))
        sent[0] += n

    def send_each(parts, remote_sem, n):
        es = engines([d for _o, _i, d in parts])[:n]
        share = n // len(parts)
        trs = []
        for j, (o_ap, i_ap, d) in enumerate(parts):
            rid, pid = topo.addr(d, core)
            trs.append(RemoteDMATransfer(dst_ids=[DstId(rid=rid, pnc=pid)],
                                         dma_engine_mask=bits(es[share * j:share * j + share]),
                                         remote_sem=remote_sem, srcs=[i_ap], dsts=[o_ap], alu_op=0))
        g.remote_dma_fused(trs, local_sem=sem.loc)
        sent[0] += share * len(parts)

    def tile_order(server_core):
        first = list(range(LAST))
        return (first if server_core in mem else first[::-1]) + [LAST]

    def lands(s, h):
        return T.land[:, SLOT * s:SLOT * s + WIN] if h == 0 else T.land[:, SLOT * s + QP:SLOT * s + QP + WIN]

    def tcol(t):
        return 128 * t + (PAD if t == LAST else 0)

    q0 = tcol(tile) + QP * half
    myq = T.qall[:, q0:q0 + QP]
    LA, NA = tcol(LAST) - 2, tcol(LAST) - 1
    lc = 0 if half == 0 else 2 * QP
    kc = lc + 1
    others = [s for s in range(2) if s != slot]

    if is_mem:
        g.sync.dma_start(T.kbuf[:], T.k[:]).then_inc(sem.ks, 16)
        g.sync.dma_start(myq, T.q[:]).then_inc(sem.qld, 16)
        g.sync.dma_start(T.vbuf[:], T.v[:]).then_inc(sem.vs, 16)
    else:
        g.sync.dma_start(myq, T.q[:]).then_inc(sem.qld, 16)
    dve.memset(T.zer[:], 0.0).then_inc(sem.zr, 1)
    act.wait_ge(sem.zr, 1)
    if is_mem:
        dve.memset(T.ones[:], 1.0).then_inc(sem.idn, 1)
        act.activation(T.qall[QP:128, LA:NA + 1], T.zer[QP:128, 0:2], AF.Exp).then_inc(sem.eZ, 1)
        g.wait_ge(sem.idn, 1)
        g.affine_select(T.ident[:], T.ones[:], [[-1, 128]], A.is_equal, 0.0, 0, 1).then_inc(sem.idd, 1)
    else:
        act.activation(T.ones[:], T.zer[:], AF.Exp).then_inc(sem.idn, 1)
    if half == 1:
        for s in others:
            dve.memset(T.land[:, SLOT * s:SLOT * s + QP], 0.0).then_inc(sem.lz, 1)

    copies = []
    if is_mem:
        copies = [server[(R2, mem.index(core))] for R2 in members if R2 != R]
        g.wait_ge(sem.ks, 16)
        for d in copies:
            send(T.kbuf[:], T.kbuf[:], d, sem.ks, NK)
    targets = sorted([d for d in srv if d != core], key=lambda d: tile_order(d).index(tile))
    g.wait_ge(sem.qld, 16)
    if is_mem:
        g.wait_ge(sem.eC, 1)
        g.wait_ge(sem.eL, 1)
        g.wait_ge(sem.eZ, 1)
    qsent = T.qall[:, LA:q0 + QP] if is_mem else myq
    for d in targets:
        send(qsent, qsent, d, sem["qa%d" % tile], NQ)
    if is_mem:
        g.wait_ge(sem.vs, 16)
        for d in copies:
            send(T.vbuf[:], T.vbuf[:], d, sem.vs, NK)
    if not is_mem:
        g.wait_ge(sem.idn, 1)
        g.affine_select(T.ident[:], T.ones[:], [[-1, 128]], A.is_equal, 0.0, 0, 1).then_inc(sem.idd, 1)

    turned_bank = {0: T.ps0, 1: T.ps1}

    if slot is not None:
        order = tile_order(core)
        o0, o1, o2 = order
        k_ready = 16 if is_mem else NK
        v_ready = 16 if is_mem else NK
        hp = 1 - half
        bank = {(o0, 0): T.pst0, (o0, 1): T.pst1, (o1, 0): T.pst2, (o1, 1): T.pst3, (o2, 0): T.pst0, (o2, 1): T.pst1}
        turned_bank = {slot: T["ps%d" % o0], 1 - slot: T["ps%d" % o1]}

        def S(t):
            for c in mine[2 * t:2 * t + 2]:
                if c == core:
                    pe.wait_ge(sem.qld, 16)
            pe.wait_ge(sem["qa%d" % t], NQ * len([c for c in mine[2 * t:2 * t + 2] if c != core]))
            pe.wait_ge(sem.ks, k_ready)
            pe.matmul(T["ps%d" % t][:, 0:KEYS], T.qall[:, tcol(t):tcol(t) + 128], T.kbuf[:], True, True
                      ).then_inc(sem["sS%d" % t], 1)

        def top(t):
            dve.wait_ge(sem["sS%d" % t], 1)
            dve.tensor_reduce(T.nb[:, t:t + 1], T["ps%d" % t][:, 0:KEYS], AxisListType.X, A.max, negate=True
                              ).then_inc(sem["sC%d" % t], 1)

        def fixed(t):
            return sem.sA if (t == LAST and not is_mem) else sem["sC%d" % t]

        def adopt(t):
            dve.wait_ge(sem["sC%d" % t], 1)
            dve.wait_ge(sem["qa%d" % t], NQ)
            dve.tensor_scalar(T.nb[0:QP, t:t + 1], T.nb[0:QP, t:t + 1], CAP, T.qall[0:QP, NA:NA + 1], A.add, A.min
                              ).then_inc(sem.sA, 1)

        def ratio_out(t):
            dve.wait_ge(sem["xE%d0" % t], 1)
            dve.wait_ge(sem["xE%d1" % t], 1)
            dve.tensor_scalar(T.lr[0:QP, 0:1], T.qall[0:QP, LA:LA + 1], T.ls[0:QP, 2 * t:2 * t + 1],
                              T.ls[0:QP, 2 * t + 1:2 * t + 2], A.add, A.add).then_inc(sem.r1, 1)
            dve.wait_ge(sem.r1, 1)
            dve.reciprocal(T.lr[0:QP, 1:2], T.lr[0:QP, 0:1]).then_inc(sem.r2, 1)
            dve.wait_ge(sem.r2, 1)
            dve.tensor_copy(T["ob%d" % t][0:QP, 0:1], T.lr[0:QP, 1:2]).then_inc(sem["sL%d" % t], 1)

        def step_out(t):
            dve.wait_ge(fixed(t), 1)
            dve.wait_ge(sem.zr, 1)
            dve.tensor_scalar(T["ob%d" % t][:, 1:2 * WIN:2 * QP + 2], T.zer[:, 0:2], T.nb[:, t:t + 1], None, A.add
                              ).then_inc(sem["sB%d" % t], 1)

        def sum_out(t):
            dve.wait_ge(sem["xE%d0" % t], 1)
            dve.wait_ge(sem["xE%d1" % t], 1)
            dve.wait_ge(sem.zr, 1)
            dve.tensor_scalar(T["ob%d" % t][:, 0:2 * WIN - 1:2 * QP + 2], T.zer[:, 0:2], T.ls[:, 2 * t:2 * t + 1],
                              T.ls[:, 2 * t + 1:2 * t + 2], A.add, A.add).then_inc(sem["sL%d" % t], 1)

        def own_cols(t):
            dve.wait_ge(fixed(t), 1)
            dve.tensor_copy(T.land[:, SLOT * slot + kc:SLOT * slot + kc + 1], T.nb[:, t:t + 1]).then_inc(sem.sBo, 1)
            dve.wait_ge(sem["xE%d0" % t], 1)
            dve.wait_ge(sem["xE%d1" % t], 1)
            dve.tensor_tensor(T.land[:, SLOT * slot + lc:SLOT * slot + lc + 1], T.ls[:, 2 * t:2 * t + 1],
                              T.ls[:, 2 * t + 1:2 * t + 2], A.add).then_inc(sem.sLo, 1)

        def expo(t, b):
            act.wait_ge(fixed(t), 1)
            act.activation(T["p%d" % t][:, 128 * b:128 * b + 128], T["ps%d" % t][:, 128 * b:128 * b + 128], AF.Exp,
                           bias=T.nb[:, t:t + 1], scale=1.0, accum_out=T.ls[:, 2 * t + b:2 * t + b + 1]
                           ).then_inc(sem["xE%d%d" % (t, b)], 1)

        def turn(t, b):
            pe.wait_ge(sem.idd, 1)
            pe.wait_ge(sem["xE%d%d" % (t, b)], 1)
            if t == o2:
                pe.wait_ge(sem["xP%d%d" % (o0, b)], 1)
            pe.transpose(bank[(t, b)][:, 0:128], T["p%d" % t][:, 128 * b:128 * b + 128], T.ident[:]
                         ).then_inc(sem["xT%d%d" % (t, b)], 1)

        def turned(t, b):
            dve.wait_ge(sem["xT%d%d" % (t, b)], 1)
            dve.tensor_copy(T["pt%d" % t][:, 128 * b:128 * b + 128], bank[(t, b)][:, 0:128]
                            ).then_inc(sem["xP%d%d" % (t, b)], 1)

        def VP(t, b):
            pe.wait_ge(sem["xP%d%d" % (t, b)], 1)
            pe.wait_ge(sem.vs, v_ready)
            lo, n = (0, 128) if t != LAST else (QP * hp, QP)
            i = pe.matmul(T["ps%d" % t][:, 256:256 + n], T.vbuf[:, 128 * b:128 * b + 128],
                          T["pt%d" % t][:, 128 * b + lo:128 * b + lo + n], b == 0, b == 1)
            if b == 1:
                i.then_inc(sem["sO%d" % t], 1)

        def PV_own(b):
            if b == 0:
                pe.wait_ge(sem["sR%d" % o0], 1)
            i = pe.matmul(turned_bank[slot][:, 0:128], T["pt%d" % LAST][:, 128 * b:128 * b + 128],
                          T.vbuf[:, 128 * b:128 * b + 128], b == 0, b == 1)
            if b == 1:
                i.then_inc(sem["tT%d" % slot], 1)

        def out(t):
            act.wait_ge(sem["sO%d" % t], 1)
            lo, n = (0, 128) if t != LAST else (QP * hp, QP)
            act.activation(T["ob%d" % t][:, 2 + lo:2 + lo + n], T["ps%d" % t][:, 256:256 + n], AF.Copy
                           ).then_inc(sem["sR%d" % t], 1)

        def out_v(t):
            dve.wait_ge(sem["sO%d" % t], 1)
            dve.tensor_copy(T["ob%d" % t][:, 2:2 + 128], T["ps%d" % t][:, 256:256 + 128]).then_inc(sem["sR%d" % t], 1)

        if is_mem:
            se = T.psm[0:QP, 256:256 + KEYS]
            pe.wait_ge(sem.ks, 16)
            pe.wait_ge(sem.qld, 16)
            pe.matmul(se, myq, T.kbuf[:], True, True).then_inc(sem.eS, 1)
            dve.wait_ge(sem.eS, 1)
            dve.tensor_reduce(T.qall[0:QP, NA:NA + 1], se, AxisListType.X, A.max, negate=True).then_inc(sem.eC, 1)
            act.wait_ge(sem.eC, 1)
            act.activation(T.pown[0:QP, :], se, AF.Exp, bias=T.qall[0:QP, NA:NA + 1], scale=1.0,
                           accum_out=T.ls[0:QP, 6:7]).then_inc(sem.eE, 1)
            dve.wait_ge(sem.eE, 1)
            dve.tensor_copy(T.qall[0:QP, LA:LA + 1], T.ls[0:QP, 6:7]).then_inc(sem.eL, 1)
            pe.wait_ge(sem.idd, 1)
            pe.wait_ge(sem.eE, 1)
            for b_ in range(2):
                pe.transpose(bank[(o1, b_)][:, 0:QP], T.pown[0:QP, 128 * b_:128 * b_ + 128], T.ident[0:QP, 0:QP]
                             ).then_inc(sem["eT%d" % b_], 1)
            for b_ in range(2):
                dve.wait_ge(sem["eT%d" % b_], 1)
                dve.tensor_copy(T.ptown[:, QP * b_:QP * b_ + QP], bank[(o1, b_)][:, 0:QP]).then_inc(sem["eP%d" % b_], 1)
            pe.wait_ge(sem.eP0, 1)
            pe.wait_ge(sem.eP1, 1)
            pe.wait_ge(sem.vs, 16)
            for b_ in range(2):
                pe.matmul(T.psm[0:QP, 0:128], T.ptown[:, QP * b_:QP * b_ + QP], T.vbuf[:, 128 * b_:128 * b_ + 128],
                          b_ == 0, False)
        else:
            dve.memset(T["ob%d" % LAST][QP:128, 0:1], 0.0).then_inc(sem["sL%d" % LAST], 1)

        S(o0); S(o1); S(o2); turn(o0, 0); turn(o0, 1); turn(o1, 0); turn(o1, 1); turn(o2, 0); turn(o2, 1)
        VP(o0, 0); VP(o0, 1); VP(o1, 0); VP(o1, 1); VP(o2, 0); VP(o2, 1)
        if not is_mem:
            PV_own(0); PV_own(1)
            pe.wait_ge(sem["sR%d" % o1], 1)
        top(o0); top(o1); top(o2)
        if not is_mem:
            adopt(o2)
        turned(o0, 0); turned(o0, 1); step_out(o0); sum_out(o0)
        turned(o1, 0); turned(o1, 1); step_out(o1); sum_out(o1)
        turned(o2, 0); turned(o2, 1); step_out(o2)
        if is_mem:
            sum_out(o2)
        else:
            ratio_out(o2); own_cols(o2)
        out_v(o1)
        expo(o0, 0); expo(o0, 1); expo(o1, 0); expo(o1, 1); expo(o2, 0); expo(o2, 1); out(o0); out(o2)

        for t in order:
            g.wait_ge(sem["sR%d" % t], 1)
            g.wait_ge(sem["sB%d" % t], 1)
            g.wait_ge(sem["sL%d" % t], 2 if (t == LAST and not is_mem) else 1)
            parts = [(lands(slot, h), T["ob%d" % t][:, WIN * h:WIN * h + WIN], c)
                     for h, c in enumerate(mine[2 * t:2 * t + 2]) if c != core]
            if len(parts) == 1:
                send(parts[0][0], parts[0][1], parts[0][2], sem["pa%d" % slot], NR)
            else:
                send_each(parts, sem["pa%d" % slot], NR)

    arrives = NR if tile == LAST else NR // 2
    p0 = QP * half

    def rows(buf, a, b, step=1):
        return buf[p0:p0 + QP, a:b:step]

    if is_mem:
        s = others[0]
        pe.wait_ge(sem["pa%d" % s], arrives)
        pe.matmul(T.psm[0:QP, 0:128], T.land[:, SLOT * s + 2:SLOT * s + 2 + QP], T.ident[:], False, True
                  ).then_inc(sem["tT%d" % s], 1)
        dve.wait_ge(sem["pa%d" % s], arrives)
        dve.wait_ge(sem["tT%d" % s], 1)
        dve.tensor_scalar(T.ybuf[0:QP, :], T.psm[0:QP, 0:128], T.land[0:QP, SLOT * s:SLOT * s + 1], None, A.mult
                          ).then_inc(sem.m9, 1)
    else:
        plain = slot is None
        np_ = QP if half == 0 else 128

        def wide(buf, a, b):
            return buf[0:np_, a:b] if plain else rows(buf, a, b)

        for s in others:
            pe.wait_ge(sem["pa%d" % s], arrives)
            pe.wait_ge(sem.idd, 1)
            opened = plain and s == 0
            if half == 0:
                i = pe.matmul(turned_bank[s][0:QP, 0:128], T.land[:, SLOT * s + 2:SLOT * s + 2 + QP], T.ident[:],
                              True, not opened)
            else:
                pe.wait_ge(sem.lz, len(others))
                i = pe.matmul(turned_bank[s][:, 0:128], T.land[:, SLOT * s:SLOT * s + 128], T.ident[:], True, not opened)
            if not opened:
                i.then_inc(sem["tT%d" % s], 1)
        for s in range(2):
            if s == slot:
                dve.wait_ge(sem.sBo, 1)
                dve.wait_ge(sem.sLo, 1)
            else:
                dve.wait_ge(sem["pa%d" % s], arrives)
        dve.tensor_scalar(wide(T.nm, 0, 1), wide(T.land, kc, kc + 1), wide(T.land, SLOT + kc, SLOT + kc + 1), CAP2,
                          A.subtract, A.min).then_inc(sem.m1, 1)
        act.wait_ge(sem.m1, 1)
        act.activation(wide(T.ab, 0, 1), wide(T.nm, 0, 1), AF.Exp).then_inc(sem.m4, 1)
        act.wait_ge(sem.m4, 1)
        act.wait_ge(sem.tT1, 1)
        act.activation(wide(T.tab if plain else T.ta, 0, 128), wide(turned_bank[1], 0, 128), AF.Copy,
                       scale=wide(T.ab, 0, 1)).then_inc(sem.mA, 1)
        dve.wait_ge(sem.m4, 1)
        dve.tensor_scalar(rows(T.lt, 0, 1), rows(T.ab, 0, 1), rows(T.land, SLOT + lc, SLOT + lc + 1),
                          rows(T.land, lc, lc + 1), A.mult, A.add).then_inc(sem.m6, 1)
        dve.wait_ge(sem.m6, 1)
        dve.reciprocal(rows(T.rr, 0, 1), rows(T.lt, 0, 1)).then_inc(sem.m7, 1)
        if plain:
            pe.wait_ge(sem.mA, 1)
            pe.matmul(turned_bank[0][0:np_, 0:128], T.ident[0:np_, 0:np_], T.tab[0:np_, 0:128], False, True
                      ).then_inc(sem.tT0, 1)
            dve.wait_ge(sem.tT0, 1)
            dve.wait_ge(sem.m7, 1)
            dve.tensor_scalar(rows(T.ybuf, 0, 128), rows(turned_bank[0], 0, 128), rows(T.rr, 0, 1), None, A.mult
                              ).then_inc(sem.m9, 1)
        else:
            dve.wait_ge(sem.mA, 1)
            dve.wait_ge(sem.tT0, 1)
            dve.tensor_tensor(rows(T.tt, 0, 128), rows(turned_bank[0], 0, 128), rows(T.ta, 0, 128), A.add
                              ).then_inc(sem.m8, 1)
            dve.wait_ge(sem.m7, 1)
            dve.wait_ge(sem.m8, 1)
            dve.tensor_scalar(rows(T.ybuf, 0, 128), rows(T.tt, 0, 128), rows(T.rr, 0, 1), None, A.mult
                              ).then_inc(sem.m9, 1)
    g.sync.wait_ge(sem.m9, 1)
    g.sync.dma_start(T.y[:], T.ybuf[p0:p0 + QP, :]).then_inc(sem.st, 16)
    g.sync.wait_ge(sem.st, 16)
    g.wait_ge(sem.loc, sent[0])
